import numpy as np, ml_dtypes
CORES = [9,25,41,57]
N = 4
import mx_ref
BF = ml_dtypes.bfloat16
def gentries(a):
    return np.ascontiguousarray(a.reshape(8, 16, -1).transpose(0, 2, 1)).reshape(8, -1)
def gtable(e):
    e = np.asarray(e); return np.ascontiguousarray(e.reshape(8, -1, 16).transpose(0, 2, 1)).reshape(128, -1).astype(np.int32)
def gcols(t, e):
    v = np.concatenate([t.reshape(8, 16, -1, 4), np.zeros((8, 16, 1, 4), BF)], axis=2)
    return np.ascontiguousarray(np.stack([v[g][:, e[g]] for g in range(8)])).reshape(128, -1)
def tile(rs):
    return np.stack(rs, axis=2).reshape(128, -1).astype(BF)
def pick(q, e):
    c = np.concatenate([q[0].reshape(128, -1, 4), np.zeros((128, 1, 4), np.uint8)], axis=1); s = np.concatenate([q[1], np.ones((16, 1), np.uint8)], axis=1)
    return (np.ascontiguousarray(c[:, e].reshape(128, -1)), np.ascontiguousarray(s[:, e]))
def join(*qs):
    return (np.concatenate([q[0] for q in qs], axis=1), np.concatenate([q[1] for q in qs], axis=1))
def put(q, e, v):
    c, s = q[0].reshape(128, -1, 4).copy(), q[1].copy(); c[:, e] = v[0].reshape(128, -1, 4); s[:, e] = v[1]
    return (c.reshape(128, -1), s)
def pk(c, s):
    return (np.ascontiguousarray(c), mx_ref.live(s))
def emit(q):
    return q[0], q[1]
def packed(v, rng):
    q = [mx_ref.quantize(np.ascontiguousarray(v[r])) for r in range(N)]
    return np.stack([a for a, b in q]), np.stack([mx_ref.plane(b, rng) for a, b in q])
def values_of_codes():
    e, c = np.zeros((128, 128, 4), np.float32), np.zeros((128, 2, 4), np.uint8)
    e[np.arange(128), np.arange(128), 0] = 1
    c[:127, :, 0] = np.arange(256).reshape(2, 128).T[:127]
    return mx_ref.matmul(mx_ref.quantize(e.reshape(128, 512).astype(BF)), (c.reshape(128, 8), np.full((16, 2), 127, np.uint8))).T.reshape(-1).astype(np.float64)
CODE_VALUE, SCALE_VALUE = values_of_codes(), 2.0 ** (np.arange(256) - 127.0)
def decode(q):
    return (CODE_VALUE[q[0]].reshape(16, 8, -1, 4) * SCALE_VALUE[q[1]][:, None, :, None] + 0.0).reshape(128, -1).astype(np.float32)
def f(rng, *shape):
    return mx_ref.flush((rng.standard_normal(shape, dtype=np.float32) * np.exp2(rng.integers(-2, 3, shape[:-1] + (1,)))).astype(BF))
def wide(rng, *shape, cols=0):
    v = rng.standard_normal(shape, dtype=np.float32) * np.exp2(rng.integers(-12, 13, shape)).astype(np.float32)
    if cols: v *= np.repeat(np.exp2(rng.integers(-cols, cols + 1, shape[:-2] + (1, shape[-1] // 4))) * (rng.random(shape[:-2] + (1, shape[-1] // 4)) > 0.0625), 4, axis=-1).astype(np.float32)
    return mx_ref.flush(v.astype(BF))
C, T, R = 320, 2560, 3
def big(v):
    v = v.astype(np.float32)
    v[np.abs(v) < np.float32(2.0 ** -12)] = 0
    return v.astype(BF)
def numbers_of(rng):
    return {"x": big(f(rng, N, 128, 4 * C)), "u": np.array(f(rng, N, 128, 512)), "v": np.array(f(rng, N, 128, 512))}
def lists_of(t):
    return np.stack([gtable(t[r]) for r in range(N)])
def layers(rng, still=[], full=False):
    w = np.zeros((N, 512, 512), np.float32)
    k = rng.random((N, 512, 512))
    k[:, :, np.isin(np.arange(512) // 4 % 16, still)] = 2
    e = np.argpartition(k, 8, axis=2)[:, :, :8]
    a = rng.integers(4, 16, (N, 512, 8)) * 0.25 * rng.choice([-1.0, 1.0], (N, 512, 8))
    if full: a = 4.0 * rng.choice([-1.0, 1.0], (N, 512, 1)) * np.ones((1, 1, 8))
    np.put_along_axis(w, e, a.astype(np.float32), axis=2)
    w[:, np.isin(np.arange(512) % 16, still)] = 0
    return w
def weights(rng, w):
    c, s = packed(np.ascontiguousarray(w.reshape(N, 512, 128, 4).transpose(0, 2, 1, 3)).reshape(N, 128, 2048).astype(BF), rng)
    return {"wc": c, "ws": s}
def setup_inputs(rng):
    return {**numbers_of(rng), "p": lists_of(rng.integers(0, T, (N, 8, C))), **weights(rng, layers(rng))}
def setup_inputs_ties(rng):
    d = numbers_of(rng)
    x = d["x"].reshape(N, 8, 16, C, 4)
    x[:, :, 0] = 0
    x[:, :, 0, :, 0] = rng.integers(0, 3, (N, 8, C)).astype(np.float32).astype(BF)
    u = d["u"].reshape(N, 128, 128, 4)
    u[:, :, ::16] = 0
    o = rng.permutation(N)
    for r in range(N):
        for h in range(0, 128, 16): u[r, h, h, 0] = 0.0 if r == o[0] else -1.0 if r == o[1] else 1.0
    t = rng.integers(0, T, (N, 8, C))
    t[o[:2]] = C * rng.integers(0, 4, (2, 8, C))
    t[o[2]] = rng.integers(0, T)
    t[o[3]] = C * (7 - np.arange(8))[:, None]
    return {"x": x.reshape(N, 128, 4 * C), "u": u.reshape(N, 128, 512), "v": d["v"], "p": lists_of(t), **weights(rng, layers(rng, [0]))}
def setup_inputs_near(rng):
    d = numbers_of(rng)
    x = d["x"].astype(np.float32).reshape(N, 8, 16, C, 4)
    x[:, :, 0] = 0
    x[:, :, 8:] = 0
    u = d["u"].reshape(N, 128, 128, 4)
    u[:, :, ::16] = 0
    t = rng.integers(0, T, (N, 8, C))
    o = rng.permutation(N) % 4
    for r in range(N):
        s = rng.integers(0, 16, (8, C))
        if o[r] == 1:
            s[5:] = np.minimum(s[5:], 12)
            s[5:, 4:9] = [15, 15, 14, 13, 12]
            t[r] = np.minimum(t[r], T - 2)
            t[r, 5, :16] = T - 1
            t[r, 6, :9] = T - 1
            t[r, 7, :7] = T - 1
        if o[r] < 3: x[r, :, 8] = ((s[:, :, None] >> np.arange(4)) & 1) * np.exp2(np.arange(4) - 22.0)
        if o[r] < 2:
            x[r, :, 0, :, 0] = rng.choice([-1.0, 1.0], (8, 1))
            x[r, :, 11, :, 0] = 2.0 ** -10
        if o[r] == 2:
            for g in rng.permutation(8)[:4]: x[r, g, 0, rng.integers(C), 0] = 2.0 ** 26 * rng.choice([-1.0, 1.0])
        if o[r] == 3:
            x[r, :, 10, :, 0] = np.where(s < 8, 1.125 * 2.0 ** -29, 0.0)
            x[r, :, 11, :, 0] = np.where(s < 8, 0.0, 2.0 ** -29)
        k = 1.0 if o[r] == 0 else 2.0 ** -30
        for h in range(0, 128, 16):
            if o[r] < 2:
                u[r, h, h, 0] = k
                u[r, h + 11, h, 0] = k
            if o[r] == 2: u[r, h, h, 0] = 2.0 ** 30
            if o[r] < 3: u[r, h + 8, h] = k
            else:
                u[r, h + 10, h, 0] = 1.125 * k
                u[r, h + 11, h, 0] = 1.25 * k
    return {"x": x.reshape(N, 128, 4 * C).astype(BF), "u": u.reshape(N, 128, 512), "v": d["v"], "p": lists_of(t), **weights(rng, layers(rng, [0, 8, 9, 10, 11, 12, 13, 14, 15]))}
def setup_inputs_fine(rng):
    d = numbers_of(rng)
    x = (1.0 + (2 * rng.integers(0, 64, (N, 8, 2, 8, C, 4)) + 1) * 2.0 ** -7) * np.exp2(-rng.integers(8, 15, (N, 8, 2, 8, C, 4))) * rng.choice([-1.0, 1.0], (N, 8, 2, 8, C, 4))
    np.put_along_axis(x[..., 0], rng.integers(0, 8, (N, 8, 2, 1, C)), 1.96875 * rng.choice([-1.0, 1.0], (N, 8, 2, 1, C)), axis=3)
    x = x * np.exp2(rng.integers(-1, 3, (N, 8, 2, 1, C, 1)))
    return {"x": x.astype(np.float32).reshape(N, 128, 4 * C).astype(BF), "u": d["u"], "v": d["v"], "p": lists_of(rng.integers(0, T, (N, 8, C))), **weights(rng, layers(rng))}
def setup_inputs_ends(rng):
    k = int(rng.integers(0, 2))
    o = np.roll(np.array([2, 3, k, 1 - k])[np.arange(N) % 4], int(rng.integers(0, N)))
    sign = np.array([1.0, -1.0, 1.0, 1.0])
    x = np.zeros((N, 8, 16, C, 4))
    u = np.array(f(rng, N, 128, 512)).reshape(N, 128, 128, 4)
    v = (rng.integers(0, 2, (N, 128, 512)) * 2.0 - 1.0) * 2.0 ** 30
    w = layers(rng, full=True)
    t = np.zeros((N, 8, C), np.int64)
    for r in range(N):
        a = 2.0 ** 26 * rng.choice([1.0, 0.875, 0.75], (8, 1, C, 1))
        if o[r] == 0: x[r] = a
        if o[r] == 1:
            x[r] = -a
            t[r] = T - 1
        if o[r] < 2:
            w[r] = np.abs(w[r]) * (sign[o[r]] * sign[o[r - 1]])
            if o[r - 1] == 3:
                w[r, :, :64] = np.sum(w[r].reshape(512, 8, 64), axis=1)
                w[r, :, 64:] = 0
        if o[r] == 2:
            x[r] = 2.0 ** -30
            w[r] = 0
            t[r] = (T - 1) * rng.integers(0, 2, (8, C))
        if o[r] == 3:
            x[r] = 2.0 ** 26 * rng.choice([-1.0, 1.0], (8, 1, C, 1))
            x[r, 0] = 2.0 ** 26
            t[r] = (T - 1) * (rng.permutation(8) % 2)[:, None]
        h = rng.permutation(6) % 2 * 2.0 - 1.0
        for g in range(8): u[r, :, 16 * g] = 0.0 if g in (0, 7) else (2.0 ** -30 if o[r] == 2 else 2.0 ** 30) * float(h[g - 1])
    v = (np.where(v < 0, -1.0, 1.0) * np.where(rng.permutation(N) % 2, 2.0 ** -30, 2.0 ** 30)[:, None, None]).astype(np.float32).astype(BF)
    return {"x": x.astype(np.float32).reshape(N, 128, 4 * C).astype(BF), "u": u.reshape(N, 128, 512), "v": v.astype(np.float32).astype(BF), "p": lists_of(t), **weights(rng, w)}
def setup_inputs_spread(rng):
    d = setup_inputs(rng)
    d["x"] = big(wide(rng, N, 128, 4 * C, cols=6))
    return d
def check_inputs(d):
    b = []
    for k, most in (("x", 2.0 ** 26), ("u", 2.0 ** 30), ("v", 2.0 ** 30)):
        a = np.abs(d[k].astype(np.float32))
        if not (np.isfinite(a).all() and ((a == 0) | (a >= 2.0 ** -30) & (a <= most)).all()): b.append("a value of " + k)
    if not ((d["p"] >= 0) & (d["p"] < T)).all(): b.append("an entry of p")
    none, least, most = [emit(mx_ref.quantize(np.full((128, 16), k, np.float32).astype(BF)))[1][0, 0] for k in (0.0, 2.0 ** -30, 2.0 ** 30)]
    for r in range(N):
        if ((d["wc"][r] == 0x7F) | (d["wc"][r] == 0xFF)).any(): b.append("wc: a code that is no number")
        s = mx_ref.live(d["ws"][r])
        if ((s != none) & ((s < least) | (s > most))).any(): b.append("ws: a scale out of range")
        a = np.abs(decode(pk(d["wc"][r], d["ws"][r])).astype(np.float64)).reshape(128, 512, 4)
        if not (np.sum(a, axis=(0, 2)) <= 32).all(): b.append("sizes in a column of W")
    return b
def order_of(t):
    place = np.argsort(np.argsort(T * t.reshape(-1) + np.arange(T))).reshape(8, C)
    o = np.argsort(place, axis=1)
    k = np.stack([np.searchsorted(place[g, o[g]], 8 * np.arange(C) + 7, side="right") for g in range(8)]) - 1
    k = np.maximum(k, 0)
    return place // 8, np.take_along_axis(o, k, axis=1), np.take_along_axis(o, np.minimum(k + 1, C - 1), axis=1)
def reference(x, u, v, p, wc, ws):
    qu = [mx_ref.quantize(u[r]) for r in range(N)]
    lay = [pk(wc[r], ws[r]) for r in range(N)]
    now = [x[r] for r in range(N)]
    pos = np.stack([gentries(p[r]) for r in range(N)]).astype(np.int64)
    for t in range(R):
        own, q = [], []
        for r in range(N):
            own.append(decode(mx_ref.quantize(now[r])).astype(BF))
            c, m, n = order_of(pos[r])
            z = ((gcols(own[r], m).astype(np.float32) + gcols(own[r], n).astype(np.float32)) * np.float32(0.5)).astype(BF)
            q.append(mx_ref.quantize(z))
            s = mx_ref.matmul(qu[r], q[r])[::16] + np.float32(0.0)
            step = np.argsort(np.argsort(s, axis=1, kind="stable"), axis=1)
            pos[r] += np.take_along_axis(step, c, axis=1)
        for r in range(N):
            came = pick(q[(r + N - 1) % N], np.arange(1, C, 2))
            h = tile([mx_ref.matmul(pick(lay[r], np.arange(128 * b, 128 * b + 128)), came) * np.float32(0.03125) for b in range(4)])
            c, m, n = order_of(pos[r])
            now[r] = (own[r].astype(np.float32) + gcols(h, c // 2).astype(np.float32)).astype(BF)
    y, pt = np.zeros((N, 128, C), np.float32), np.zeros((N, 8, C), np.float32)
    oc, osc = np.zeros((N, 128, 4 * C), np.uint8), np.zeros((N, 16, C), np.uint8)
    for r in range(N):
        q = mx_ref.quantize(now[r])
        y[r] = mx_ref.matmul(mx_ref.quantize(v[r]), q)
        pt[r] = pos[r]
        oc[r], osc[r] = emit(q)
    return {"y": y, "pt": pt, "oc": oc, "osc": osc}

@@ -1,0 +1,403 @@
+from concourse.mybir import dt, AluOpType as A, ActivationFunctionType as F
+
+C, P, R = 320, 128, 3
+NV = 3520
+NULL = 3528
+WW = 3936
+NS = 11
+BIG = 4194304.0
+
+SCRATCH, AT = {}, {}
+
+
+def _b(n, w, d="float32", where="sbuf"):
+    SCRATCH[n] = (where, [P, w], d)
+    AT[n] = (n, 0, w)
+
+
+def _t(n, d, parts, where="sbuf"):
+    a = 0
+    for k, w in parts:
+        AT[k] = (n, a, w)
+        a += w
+    SCRATCH[n] = (where, [P, a], d)
+
+
+for _n, _w in (("E16", C), ("JR", C), ("T17", 340), ("E32", 640), ("TNY", 1), ("MASK", C), ("MSKA", C), ("RS", C), ("RS32", 640), ("MB0", 340),
+               ("MB", 340), ("KF0", C), ("KFA", C), ("KFB", C), ("KM", C), ("KS", C), ("SK", 352), ("S1", 340), ("S2", 340), ("GS", 640),
+               ("OWD", 336), ("O2", C), ("O3", C), ("IX", 340), ("MN", C), ("MM", C), ("MS", C), ("SM", C), ("SS", C), ("DD", C), ("DM", C),
+               ("RA", C), ("STEP", C), ("PT0", C), ("PT1", C), ("YB", C)):
+    _b(_n, _w)
+_t("CTAB", "float32", [("C16", 20), ("C1", 20), ("QP", 4), ("Q20", 4), ("ODD", 4), ("EVN", 4), ("NO", 4), ("NE", 4), ("DUMP", 20)])
+_t("FTAB", "float32", [("ACC", 20), ("RK", 20), ("O17", 20), ("DU", 20), ("DT", 20), ("OW", 20), ("PLF", 20), ("P2", 20)])
+_t("VSB", "float32", [("VS%d" % k, 160) for k in range(20 - NS)])
+_t("CTABI", "int32", [("QI", 4), ("QA", 4), ("QB", 4)])
+_t("ITAB", "int32", [("KI", 20), ("PI", 20), ("K1", 20), ("SI", 40), ("SH", 40), ("PL", 20), ("CI", 20), ("C2I", 20), ("K7", 20), ("T8", 20),
+                     ("MI", 20), ("MJ", 20), ("NJ", 20)])
+_t("UTAB", "uint16", [("OQ", 40)] + [(k, 20) for k in ("PERM", "RU", "RP", "OWU", "COFF", "C2OFF", "P2U", "IXU", "MOFF", "NOFF")])
+_b("UI", 8, "int32")
+_b("PR", C, "int32")
+_b("UL", 8, "uint16")
+for _n, _w in (("ZER", 512), ("ONE", 512), ("OB1", 512), ("OB2", 512), ("CDF", C), ("ONES", C), ("UT", 512), ("VT", 512), ("X", 4 * C),
+               ("Z", 4 * C), ("W", WW), ("CC", NV), ("D", 3536), ("G", 640), ("GT", 640), ("W2", 2736), ("N2", 1360)):
+    _b(_n, _w, "bfloat16")
+_t("JUNK", "bfloat16", [("JUNK%d" % k, C) for k in range(NS)])
+_t("CMPB", "bfloat16", [("CMP%d" % k, C) for k in range(20 - NS)])
+_t("EBB", "bfloat16", [("EB%d" % k, 512) for k in range(4)])
+for _n, _w in (("FH", C), ("FF", C), ("GB", C), ("HB", 160)):
+    _t(_n + "B", "bfloat16", [("%s%d" % (_n, k), _w) for k in range(4)])
+_t("CTB", "bfloat16", [("CT%d" % k, 4 * C) for k in range(5)])
+_t("PFB", "float32", [("PF%d" % k, 512) for k in range(4)], "psum")
+_b("PS", 512, "float32", "psum")
+_b("PK", 512, "float32", "psum")
+for _n, _w in [("OB", P), ("U", P), ("UR", P), ("V", P), ("L", 512), ("X", C)] + [("%s%d" % (z, k), C) for k in range(R) for z in "ZA"]:
+    _b("q" + _n, _w, "float8_e4m3fn_x4")
+    _b("s" + _n, _w, "uint8")
+for _n, _d in (("q", "float8_e4m3fn_x4"), ("s", "uint8")):
+    _t(_n + "EB", _d, [("%sE%d" % (_n, k), P) for k in range(4)])
+    _t(_n + "CB", _d, [("%sC%d" % (_n, k), C) for k in range(5)])
+PSUM = ["PF0", "PF1", "PF2", "PF3", "PS", "PK"]
+
+SEMAPHORES = ["cv", "cs", "ct", "cg", "dp", "dx", "du", "dv", "dw", "dd", "dout", "dpt", "dy", "sent"] + ["arr%d" % k for k in range(R)]
+
+
+def region(s):
+    f = s.split("@")[0].split(":")
+    if len(f) < 3 or "@" in s:
+        return f[0], range(AT[f[0]][2])
+    return f[0], range(int(f[1]), int(f[2]), int((f + [1])[3]))
+
+
+def meet(a, b):
+    if a[-1] < b[0] or b[-1] < a[0]:
+        return False
+    return a.step == 1 or b.step == 1 or a.step != b.step or (a[0] - b[0]) % a.step == 0
+
+
+def rank_program(g, core, T, topo):
+    rank = T.rank_of(core)
+    if rank is None:
+        return
+    nxt = T.cores[(rank + 1) % len(T.cores)]
+    V, S, TE = g.vector, g.scalar, g.tensor
+    eng = {"v": V, "s": S, "t": TE, "g": g, "y": g.sync}
+    cnt, seen, wr, rd = {}, {e: {} for e in eng}, {}, {}
+
+    def ap(s):
+        s, _x, by = s.partition("@")
+        n, o, w = AT[s.split(":")[0]]
+        r = region(s)[1]
+        a, e = o + r.start, o + r.stop
+        v = T[n][:, a:e:r.step] if r.step > 1 else T[n][:, a:e]
+        return v.indirect(ap(by)) if by else v
+
+    def wait(e, deps):
+        most = {}
+        for s, n in deps:
+            most[s] = max(most.get(s, 0), n)
+        for s, n in most.items():
+            if seen[e].get(s, 0) < n:
+                eng[e].wait_ge(T.sem[s], n)
+                seen[e][s] = n
+
+    def deps_of(outs, ins, own):
+        d = []
+        for k, r in ins:
+            d += [x[1:] for x in wr.get(k, []) if meet(x[0], r)]
+            if k in PSUM:
+                d += [x[1:] for x in rd.get(k, []) if x[1] != own]
+        for k, r in outs:
+            for x in wr.get(k, []) + rd.get(k, []):
+                if (meet(x[0], r) or k in PSUM) and not (own == "ct" and x[1] == own):
+                    d.append(x[1:])
+        return d
+
+    def note(outs, ins, sem, n):
+        for k, r in ins:
+            rd[k] = [x for x in rd.get(k, []) if x[1] != sem or x[0] != r] + [(r, sem, n)]
+        for k, r in outs:
+            keep = [] if len(r) == AT[k][2] or k in PSUM else [x for x in wr.get(k, []) if x[0] != r]
+            wr[k] = keep + [(r, sem, n)]
+            if len(r) == AT[k][2] or k in PSUM:
+                rd[k] = []
+
+    def op(e, call, outs, ins, extra=()):
+        own = "c" + e
+        lists = [s.split("@")[1] for s in list(outs) + list(ins) if "@" in s]
+        o, i = [region(s) for s in outs], [region(s) for s in list(ins) + lists]
+        wait(e, deps_of(o, i, own) + list(extra))
+        cnt[own] = cnt.get(own, 0) + 1
+        call().then_inc(T.sem[own], 1)
+        note(o, i, own, cnt[own])
+
+    def dma(sem, moves, outs, ins):
+        o, i = [region(s) for s in outs], [region(s) for s in ins]
+        d = deps_of(o, i, "")
+        for q, to, fr in moves:
+            wait(q, d)
+            eng[q].dma_start(to, fr).then_inc(T.sem[sem], 16)
+            cnt[sem] = cnt.get(sem, 0) + 16
+        note(o, i, sem, cnt[sem])
+
+    def ts(o, i, s1, op0, s2=None, op1=None):
+        a1, a2 = [ap(s) if isinstance(s, str) else s for s in (s1, s2)]
+        names = [i] + [s for s in (s1, s2) if isinstance(s, str)]
+        if op1 is None:
+            op("v", lambda: V.tensor_scalar(ap(o), ap(i), a1, None, op0), [o], names)
+        else:
+            op("v", lambda: V.tensor_scalar(ap(o), ap(i), a1, a2, op0, op1), [o], names)
+
+    def tt(o, a, b, o2):
+        op("v", lambda: V.tensor_tensor(ap(o), ap(a), ap(b), o2), [o], [a, b])
+
+    def cp(o, i):
+        op("v", lambda: V.tensor_copy(ap(o), ap(i)), [o], [i])
+
+    def scan(o, a, b, init, op0, op1):
+        op("v", lambda: V.tensor_tensor_scan(ap(o), ap(a), ap(b), init, op0, op1), [o], [a, b])
+
+    def fill(n, c):
+        op("v", lambda: V.memset(ap(n), c), [n], [])
+
+    def quant(q, t):
+        op("v", lambda: V.quantize_mx(ap("q" + q), ap("s" + q), ap(t)), ["q" + q, "s" + q], [t])
+
+    def mm(ps, a, a0, b, start=True, stop=True, extra=()):
+        r = ":%d:%d" % (a0, a0 + P)
+        i = ["q" + a + r, "s" + a + r, "q" + b, "s" + b]
+        op("t", lambda: TE.matmul_mx(ap(ps + ":0:320"), ap(i[0]), ap(i[1]), ap(i[2]), ap(i[3]), start, stop), [ps], i, extra)
+
+    def act(o, i, f, acc=None, bias=None, scale=None):
+        kw = {}
+        if bias is not None:
+            kw["bias"] = ap(bias)
+        if scale is not None:
+            kw["scale"] = scale
+        if acc is not None:
+            kw["accum_out"] = ap(acc)
+        op("s", lambda: S.activation(ap(o), ap(i), f, **kw), [o] + [s for s in (acc,) if s], [i] + [s for s in (bias,) if s])
+
+    def iota(n, pattern, cm=0):
+        kw = {} if SCRATCH[AT[n.split(":")[0]][0]][2] == "int32" else {"allow_small_or_imprecise_dtypes": True}
+        op("g", lambda: g.iota(ap(n), pattern, 0, cm, **kw), [n], [])
+
+    def sel(o, i, pattern, cop, c, base, cm):
+        op("g", lambda: g.affine_select(ap(o), ap(i), pattern, cop, c, base, cm), [o], [i])
+
+    dma("dp", [("ys"[k % 2], T.PR[k:P:16, :], T.p[:, :]) for k in range(16)], ["PR"], [])
+    dma("dx", [("y", T.X[:, :], T.x[:, :])], ["X"], [])
+    dma("du", [("y", T.UT[:, :], T.u[:, :])], ["UT"], [])
+    dma("dw", [("y", T.qL[:, 0:512].bitcast(dt.uint8), T.wc[:, :]), ("y", T.sL[:, 0:512], T.ws[:, :])], ["qL", "sL"], [])
+    dma("dv", [("y", T.VT[:, :], T.v[:, :])], ["VT"], [])
+
+    iota("QI:0:2", [[0, 2]], 1)
+    iota("C1", [[1, 20]])
+    iota("JR", [[1, C]])
+    iota("E16", [[0, 20], [1, 16]])
+    iota("C16", [[16, 20]])
+    iota("T17", [[0, 20], [1, 17]])
+    iota("E32", [[0, 20], [1, 32]])
+    iota("UI", [[16, 8]])
+    ts("QA:0:2", "QI:0:2", 15, A.bitwise_and)
+    ts("QB:0:2", "QI:0:2", 4, A.arith_shift_right, 1, A.bitwise_and)
+    cp("QP:0:1", "QA:0:1")
+    cp("ODD:0:1", "QB:0:1")
+    ts("Q20:0:1", "QP:0:1", 20.0, A.mult)
+    ts("PERM", "C1", "Q20:0:1", A.add)
+    ts("MASK", "E16", "QP:0:1", A.is_equal)
+    ts("RS", "E16", 0.0, A.is_gt)
+    ts("EVN:0:1", "ODD:0:1", -1.0, A.mult, 1.0, A.add)
+    ts("NO:0:1", "ODD:0:1", float(NULL), A.mult)
+    ts("NE:0:1", "EVN:0:1", float(NULL), A.mult)
+    fill("ZER", 0.0)
+    fill("ONE", 1.0)
+    for b in range(4):
+        sel("EB%d" % b, "ZER", [[1, 512]], A.not_equal, 1.0, -b, -4)
+    sel("OB1", "ONE", [[-16, 8], [0, 64]], A.is_ge, 0.0, 0, 1)
+    sel("OB2", "OB1", [[16, 8], [0, 64]], A.is_ge, 0.0, 15, -1)
+    cp("KF0", "PR@PERM")
+    ts("KFB", "KF0", 512.0, A.mult, 512.0, A.add)
+    tt("KFA", "KFB", "JR", A.add)
+
+    def unpack():
+        for b in range(4):
+            mm("PF%d" % b, "E%d" % b, 0, "X")
+        for b in range(4):
+            act("FH%d" % b, "PF%d:0:320" % b, F.Copy, scale=0.5)
+
+    def consts_early():
+        ts("MB0", "T17", "QP:0:1", A.is_le)
+        ts("MB", "MB0", 2.0 * BIG, A.mult, -BIG, A.add)
+        ts("DUMP", "C16", "QP:0:1", A.add, 3600.0, A.add)
+        ts("CDF", "JR", -159.0, A.add)
+        fill("SK", 3600.0 * 512.0)
+        fill("W", -160.0)
+        fill("D", 0.0)
+
+    def consts_late():
+        for b in range(4):
+            quant("E%d" % b, "EB%d" % b)
+        quant("X", "X")
+        unpack()
+        ts("RS32", "E32", 0.0, A.is_gt)
+        cp("UL", "UI")
+        quant("U", "UT")
+        op("v", lambda: V.tensor_copy(T.qUR[:, 0:P].bitcast(dt.uint32), T.qU[:, 0:P].bitcast(dt.uint32).indirect(T.UL[:, 0:8])), ["qUR"], ["qU", "UL"])
+        cp("sUR", "sU@UL")
+        quant("OB", "OB2")
+        fill("ONES", 1.0)
+        fill("TNY", 2.0 ** -126)
+        ts("MSKA", "E16", "QP:0:1", A.is_le)
+
+    def half(k):
+        scan("VS%d" % k, "CMP%d:0:160" % k, "CMP%d:160:320" % k, 0.0, A.add, A.add)
+
+    def order(kf, joined, early, during, scalar_tail):
+        tt("KM", kf, "MASK", A.mult)
+        scan("KS", "RS", "KM", 0.0, A.mult, A.add)
+        for c in range(NS):
+            act("JUNK%d" % c, kf, F.Sign, acc="ACC:%d:%d" % (c, c + 1), bias="KS:%d:%d" % (16 * c + 15, 16 * c + 16), scale=-1.0)
+        n = 20 - NS
+        for k in range(n):
+            c = NS + k
+            ts("CMP%d" % k, kf, "KS:%d:%d" % (16 * c + 15, 16 * c + 16), A.is_lt)
+            if k:
+                half(k - 1)
+        cp("KI", "KS:15:320:16")
+        half(n - 1)
+        ts("PI", "KI", 9, A.arith_shift_right)
+        early()
+        ts("OQ:0:40:2", "PI", "EVN:0:1", A.mult, "NO:0:1", A.add)
+        ts("OQ:1:40:2", "PI", "ODD:0:1", A.mult, "NE:0:1", A.add)
+        op("v", lambda: V.tensor_copy(ap("RK:%d:20" % NS), T.VSB[:, 159:160 * n:160]), ["RK:%d:20" % NS], ["VS%d" % k for k in range(n)])
+        ts("RK:0:%d" % NS, "ACC:0:%d" % NS, 319.0, A.add, 0.5, A.mult)
+        ts("K1", "RK", 0.0625, A.mult, 0.53125, A.add)
+        tt("O17", "RK", "K1", A.add)
+        cp("RP", "O17")
+        cp("SK@RP", kf)
+        cp("SK:17:340:17", "SK:18:341:17")
+        scan("S1", "SK:0:340", "MB", 0.0, A.min, A.max)
+        scan("S2", "SK:1:341", "MB", 0.0, A.min, A.max)
+        cp("SI:0:20", "S1:16:340:17")
+        cp("SI:20:40", "S2:16:340:17")
+        ts("SH", "SI", 9, A.arith_shift_right)
+        tt("DU", "SH:0:20", "SH:20:40", A.is_equal)
+        tt("DT", "DU", "DUMP", A.mult)
+        tt("OW", "DT", "SH:0:20", A.max)
+        cp("OWU", "OW")
+        cp("W@OWU", "CDF")
+        scan("CC", "W:0:%d" % NV, "W:0:%d" % NV, -160.0, A.max, A.max)
+        moves = []
+        for h in range(8):
+            if h < 7:
+                moves.append((T.D[16 * (h + 1) + h:P:16, 0:NV], T.CC[16 * h:16 * h + 7 - h, 0:NV]))
+            if h:
+                moves.append((T.D[h:16 * h:16, 1:NV], T.CC[16 * h + 8:16 * h + 8 + h, 0:NV - 1]))
+        dma("dd", [("ys"[k % 2], o, i) for k, (o, i) in enumerate(moves)], ["D"], ["CC"])
+        scalar_tail()
+        if joined:
+            cp("RU", "RK")
+            cp("OWD@RU", "JR")
+            cp("OWD:320:321", "OWD:319:320")
+            ts("O2", "OWD:0:320", 512.0, A.mult)
+            tt("O3", "O2", "OWD:1:321", A.add)
+            fill("W2", 0.0)
+            fill("W", -160.0)
+        during()
+        cp("G", "D@OQ")
+        op("v", lambda: V.transpose(ap("GT"), ap("G")), ["GT"], ["G"])
+        scan("GS", "RS32", "GT", 0.0, A.mult, A.add)
+        tt("PLF", "GS:31:640:32", "RK", A.add)
+        ts("PL", "PLF", 1120.0, A.add)
+        ts("C2I", "PL", 4, A.arith_shift_right)
+        cp("C2OFF", "C2I")
+
+    def lists():
+        ts("K7", "PL", 7, A.arith_shift_right)
+        ts("T8", "K7", 8.0, A.mult, 8.0, A.add)
+        tt("P2", "T8", "PL", A.add)
+        cp("P2U", "P2")
+        cp("W2@P2U", "ONES")
+        scan("N2", "W2:0:2720:2", "W2:1:2720:2", -160.0, A.add, A.add)
+        scan("IX", "N2:3:1360:4", "MB", 0.0, A.min, A.max)
+        ts("IXU", "IX:16:340:17", 159.0, A.add, 0.0, A.max)
+        cp("MN", "O3@IXU")
+        tt("MM", "MN", "MASK", A.mult)
+        scan("MS", "RS", "MM", 0.0, A.mult, A.add)
+        cp("MI", "MS:15:320:16")
+        ts("MJ", "MI", 9, A.arith_shift_right)
+        ts("NJ", "MI", 511, A.bitwise_and)
+        cp("MOFF", "MJ")
+        cp("NOFF", "NJ")
+        ts("CI", "PL", 3, A.arith_shift_right)
+        cp("COFF", "CI")
+
+    fill("OWD", 0.0)
+    order("KFA", True, consts_early, consts_late, lambda: None)
+    names = ["KFA", "KFB"]
+    for t in range(R):
+        last = t == R - 1
+        lists()
+        qz = "Z%d" % t
+        for b in range(4):
+            act("GB%d" % b, "FH%d@MOFF" % b, F.Copy)
+        for b in range(4):
+            tt("Z:%d:1280:4" % b, "FH%d@NOFF" % b, "GB%d" % b, A.add)
+        quant(qz, "Z")
+        wait("g", [x[1:] for x in wr["q" + qz] + wr["s" + qz]])
+        rid, pid, _s = topo.addr(nxt)
+        m, arr = topo.mask(core, nxt), "arr%d" % t
+        n = 2 * len(topo.engines(core, nxt))
+        g.remote_dma(T["qA%d" % t][:, 0:C].bitcast(dt.uint8), T["q" + qz][:, 0:C].bitcast(dt.uint8), T.sem[arr], T.sem.sent, pid, rid, m)
+        g.remote_dma(T["sA%d" % t][:, 0:C], T["s" + qz][:, 0:C], T.sem[arr], T.sem.sent, pid, rid, m)
+        cnt["sent"], cnt[arr] = cnt.get("sent", 0) + n, n
+        mm("PS", "UR", 0, qz)
+        tt("SM", "PS:0:320", "MASK", A.mult)
+        act("DD", "PS:0:320", F.Abs, bias="TNY", scale=1.01 * 2.0 ** -24)
+        scan("SS", "RS", "SM", 0.0, A.mult, A.add)
+        tt("DM", "DD", "MSKA", A.mult)
+        tt("RA", "PS:0:320", "DM", A.subtract)
+        for b in range(4):
+            act("FF%d" % b, "PF%d:0:320" % b, F.Copy)
+        for w in range(5):
+            for e in range(4):
+                a = 4 * w + e
+                s, ct = "SS:%d:%d" % (16 * a + 15, 16 * a + 16), "CT%d:%%d:%%d:4" % w
+                if a:
+                    ts(ct % (e, 64 * a), "PS:0:%d" % (16 * a), s, A.is_gt)
+                ts(ct % (64 * a + e, 64 * a + 64), "RA:%d:%d" % (16 * a, 16 * a + 16), s, A.is_ge)
+                if a < 19:
+                    ts(ct % (64 * a + 64 + e, 4 * C), "PS:%d:320" % (16 * a + 16), s, A.is_ge)
+            quant("C%d" % w, "CT%d" % w)
+            mm("PK", "OB", 0, "C%d" % w, w == 0, w == 4)
+        act("STEP", "PK:0:320", F.Copy, scale=512.0)
+        old, new = names[t % 2], names[(t + 1) % 2]
+        tt(new, "STEP@COFF", old, A.add)
+
+        def deal(t=t, arr=arr):
+            for b in range(4):
+                mm("PF%d" % b, "L", P * b, "A%d" % t, extra=[(arr, cnt[arr])])
+            for b in range(4):
+                act("HB%d" % b, "PF%d:1:320:2" % b, F.Copy, scale=0.03125)
+
+        def final(new=new):
+            if last:
+                tt("PT0", new, "JR", A.subtract)
+                ts("PT1", "PT0", 2.0 ** -9, A.mult, -1.0, A.add)
+                quant("V", "VT")
+
+        order(new, not last, lambda: None, final, deal)
+        if last:
+            dma("dpt", [("y", T.pt[:, :], T.PT1[0:P:16, :])], [], ["PT1"])
+        for b in range(4):
+            tt("X:%d:1280:4" % b, "HB%d@C2OFF" % b, "FF%d" % b, A.add)
+        quant("X", "X")
+        if not last:
+            unpack()
+
+    mm("PS", "V", 0, "X")
+    dma("dout", [("y", T.oc[:, :], T.qX[:, 0:C].bitcast(dt.uint8))] +
+        [("ys"[k % 2], T.osc[4 * k:4 * k + 4, :], T.sX[32 * k:32 * k + 4, 0:C]) for k in range(4)], [], ["qX", "sX"])
+    act("YB", "PS:0:320", F.Copy)
+    dma("dy", [("s", T.y[:, :], T.YB[:, :])], [], ["YB"])
+    wait("g", list(cnt.items()))

@@ -4,7 +4,9 @@ C, P, R = 320, 128, 3
 NV = 3520
 NULL = 3528
 WW = 3936
-NS = 11
+NS = 12
+WS = 3
+CS = 64 * WS
 BIG = 4194304.0
 
 SCRATCH, AT = {}, {}
@@ -26,7 +28,7 @@ def _t(n, d, parts, where="sbuf"):
 for _n, _w in (("E16", C), ("JR", C), ("T17", 340), ("E32", 640), ("TNY", 1), ("MASK", C), ("MSKA", C), ("RS", C), ("RS32", 640), ("MB0", 340),
                ("MB", 340), ("KF0", C), ("KFA", C), ("KFB", C), ("KM", C), ("KS", C), ("SK", 352), ("S1", 340), ("S2", 340), ("GS", 640),
                ("OWD", 336), ("O2", C), ("O3", C), ("IX", 340), ("MN", C), ("MM", C), ("MS", C), ("SM", C), ("SS", C), ("DD", C), ("DM", C),
-               ("RA", C), ("STEP", C), ("PT0", C), ("PT1", C), ("YB", C)):
+               ("RA", C), ("NM", C - CS), ("ND", C - CS), ("STEP", C), ("PT0", C), ("PT1", C), ("YB", C)):
     _b(_n, _w)
 _t("CTAB", "float32", [("C16", 20), ("C1", 20), ("QP", 4), ("Q20", 4), ("ODD", 4), ("EVN", 4), ("NO", 4), ("NE", 4), ("DUMP", 20)])
 _t("FTAB", "float32", [("ACC", 20), ("RK", 20), ("O17", 20), ("DU", 20), ("DT", 20), ("OW", 20), ("PLF", 20), ("P2", 20)])
@@ -49,6 +51,7 @@ for _n, _w in (("FH", C), ("FF", C), ("GB", C), ("HB", 160)):
 _t("CTB", "bfloat16", [("CT%d" % k, 4 * C) for k in range(5)])
 _t("PFB", "float32", [("PF%d" % k, 512) for k in range(4)], "psum")
 _b("PS", 512, "float32", "psum")
+_b("PSB", 512, "float32", "psum")
 _b("PK", 512, "float32", "psum")
 for _n, _w in [("OB", P), ("U", P), ("UR", P), ("V", P), ("L", 512), ("X", C)] + [("%s%d" % (z, k), C) for k in range(R) for z in "ZA"]:
     _b("q" + _n, _w, "float8_e4m3fn_x4")
@@ -56,7 +59,7 @@ for _n, _w in [("OB", P), ("U", P), ("UR", P), ("V", P), ("L", 512), ("X", C)] +
 for _n, _d in (("q", "float8_e4m3fn_x4"), ("s", "uint8")):
     _t(_n + "EB", _d, [("%sE%d" % (_n, k), P) for k in range(4)])
     _t(_n + "CB", _d, [("%sC%d" % (_n, k), C) for k in range(5)])
-PSUM = ["PF0", "PF1", "PF2", "PF3", "PS", "PK"]
+PSUM = ["PF0", "PF1", "PF2", "PF3", "PS", "PSB", "PK"]
 
 SEMAPHORES = ["cv", "cs", "ct", "cg", "dp", "dx", "du", "dv", "dw", "dd", "dout", "dpt", "dy", "sent"] + ["arr%d" % k for k in range(R)]
 
@@ -116,10 +119,10 @@ def rank_program(g, core, T, topo):
         for k, r in ins:
             rd[k] = [x for x in rd.get(k, []) if x[1] != sem or x[0] != r] + [(r, sem, n)]
         for k, r in outs:
-            keep = [] if len(r) == AT[k][2] or k in PSUM else [x for x in wr.get(k, []) if x[0] != r]
-            wr[k] = keep + [(r, sem, n)]
-            if len(r) == AT[k][2] or k in PSUM:
-                rd[k] = []
+            whole = len(r) == AT[k][2] or k in PSUM
+            wr[k] = ([] if whole else [x for x in wr.get(k, []) if x[0] != r]) + [(r, sem, n)]
+            if whole:
+                rd[k] = [x for x in rd.get(k, []) if x[2] == n and x[1] == sem]
 
     def op(e, call, outs, ins, extra=()):
         own = "c" + e
@@ -177,9 +180,9 @@ def rank_program(g, core, T, topo):
             kw["accum_out"] = ap(acc)
         op("s", lambda: S.activation(ap(o), ap(i), f, **kw), [o] + [s for s in (acc,) if s], [i] + [s for s in (bias,) if s])
 
-    def iota(n, pattern, cm=0):
+    def iota(n, pattern, base=0, cm=0):
         kw = {} if SCRATCH[AT[n.split(":")[0]][0]][2] == "int32" else {"allow_small_or_imprecise_dtypes": True}
-        op("g", lambda: g.iota(ap(n), pattern, 0, cm, **kw), [n], [])
+        op("g", lambda: g.iota(ap(n), pattern, base, cm, **kw), [n], [])
 
     def sel(o, i, pattern, cop, c, base, cm):
         op("g", lambda: g.affine_select(ap(o), ap(i), pattern, cop, c, base, cm), [o], [i])
@@ -190,31 +193,38 @@ def rank_program(g, core, T, topo):
     dma("dw", [("y", T.qL[:, 0:512].bitcast(dt.uint8), T.wc[:, :]), ("y", T.sL[:, 0:512], T.ws[:, :])], ["qL", "sL"], [])
     dma("dv", [("y", T.VT[:, :], T.v[:, :])], ["VT"], [])
 
-    iota("QI:0:2", [[0, 2]], 1)
+    iota("QI:0:2", [[0, 2]], 0, 1)
     iota("C1", [[1, 20]])
-    iota("JR", [[1, C]])
     iota("E16", [[0, 20], [1, 16]])
-    iota("C16", [[16, 20]])
+    iota("JR", [[1, C]])
     iota("T17", [[0, 20], [1, 17]])
-    iota("E32", [[0, 20], [1, 32]])
-    iota("UI", [[16, 8]])
+    iota("C16", [[16, 20]])
+    fill("D", 0.0)
     ts("QA:0:2", "QI:0:2", 15, A.bitwise_and)
     ts("QB:0:2", "QI:0:2", 4, A.arith_shift_right, 1, A.bitwise_and)
     cp("QP:0:1", "QA:0:1")
     cp("ODD:0:1", "QB:0:1")
     ts("Q20:0:1", "QP:0:1", 20.0, A.mult)
     ts("PERM", "C1", "Q20:0:1", A.add)
-    ts("MASK", "E16", "QP:0:1", A.is_equal)
-    ts("RS", "E16", 0.0, A.is_gt)
     ts("EVN:0:1", "ODD:0:1", -1.0, A.mult, 1.0, A.add)
     ts("NO:0:1", "ODD:0:1", float(NULL), A.mult)
     ts("NE:0:1", "EVN:0:1", float(NULL), A.mult)
+    ts("MASK", "E16", "QP:0:1", A.is_equal)
+    ts("RS", "E16", 0.0, A.is_gt)
+    ts("MB0", "T17", "QP:0:1", A.is_le)
+    ts("CDF", "JR", -159.0, A.add)
+    fill("SK", 3600.0 * 512.0)
+    ts("MB", "MB0", 2.0 * BIG, A.mult, -BIG, A.add)
+    ts("DUMP", "C16", "QP:0:1", A.add, 3600.0, A.add)
     fill("ZER", 0.0)
     fill("ONE", 1.0)
     for b in range(4):
         sel("EB%d" % b, "ZER", [[1, 512]], A.not_equal, 1.0, -b, -4)
+    iota("E32", [[0, 20], [1, 32]])
+    iota("UI", [[16, 8]])
     sel("OB1", "ONE", [[-16, 8], [0, 64]], A.is_ge, 0.0, 0, 1)
     sel("OB2", "OB1", [[16, 8], [0, 64]], A.is_ge, 0.0, 15, -1)
+    iota("W2", [[0, 2736]])
     cp("KF0", "PR@PERM")
     ts("KFB", "KF0", 512.0, A.mult, 512.0, A.add)
     tt("KFA", "KFB", "JR", A.add)
@@ -224,15 +234,6 @@ def rank_program(g, core, T, topo):
             mm("PF%d" % b, "E%d" % b, 0, "X")
         for b in range(4):
             act("FH%d" % b, "PF%d:0:320" % b, F.Copy, scale=0.5)
-
-    def consts_early():
-        ts("MB0", "T17", "QP:0:1", A.is_le)
-        ts("MB", "MB0", 2.0 * BIG, A.mult, -BIG, A.add)
-        ts("DUMP", "C16", "QP:0:1", A.add, 3600.0, A.add)
-        ts("CDF", "JR", -159.0, A.add)
-        fill("SK", 3600.0 * 512.0)
-        fill("W", -160.0)
-        fill("D", 0.0)
 
     def consts_late():
         for b in range(4):
@@ -252,7 +253,7 @@ def rank_program(g, core, T, topo):
     def half(k):
         scan("VS%d" % k, "CMP%d:0:160" % k, "CMP%d:160:320" % k, 0.0, A.add, A.add)
 
-    def order(kf, joined, early, during, scalar_tail):
+    def order(kf, joined, nv, early, during, scalar_tail):
         tt("KM", kf, "MASK", A.mult)
         scan("KS", "RS", "KM", 0.0, A.mult, A.add)
         for c in range(NS):
@@ -286,23 +287,22 @@ def rank_program(g, core, T, topo):
         tt("OW", "DT", "SH:0:20", A.max)
         cp("OWU", "OW")
         cp("W@OWU", "CDF")
-        scan("CC", "W:0:%d" % NV, "W:0:%d" % NV, -160.0, A.max, A.max)
+        scan("CC:0:%d" % nv, "W:0:%d" % nv, "W:0:%d" % nv, -160.0, A.max, A.max)
         moves = []
         for h in range(8):
             if h < 7:
-                moves.append((T.D[16 * (h + 1) + h:P:16, 0:NV], T.CC[16 * h:16 * h + 7 - h, 0:NV]))
+                moves.append((T.D[16 * (h + 1) + h:P:16, 0:nv], T.CC[16 * h:16 * h + 7 - h, 0:nv]))
             if h:
-                moves.append((T.D[h:16 * h:16, 1:NV], T.CC[16 * h + 8:16 * h + 8 + h, 0:NV - 1]))
+                moves.append((T.D[h:16 * h:16, 1:nv], T.CC[16 * h + 8:16 * h + 8 + h, 0:nv - 1]))
         dma("dd", [("ys"[k % 2], o, i) for k, (o, i) in enumerate(moves)], ["D"], ["CC"])
         scalar_tail()
         if joined:
+            iota("W", [[0, WW]], -160)
             cp("RU", "RK")
             cp("OWD@RU", "JR")
             cp("OWD:320:321", "OWD:319:320")
             ts("O2", "OWD:0:320", 512.0, A.mult)
             tt("O3", "O2", "OWD:1:321", A.add)
-            fill("W2", 0.0)
-            fill("W", -160.0)
         during()
         cp("G", "D@OQ")
         op("v", lambda: V.transpose(ap("GT"), ap("G")), ["GT"], ["G"])
@@ -312,13 +312,15 @@ def rank_program(g, core, T, topo):
         ts("C2I", "PL", 4, A.arith_shift_right)
         cp("C2OFF", "C2I")
 
-    def lists():
+    def lists(again):
         ts("K7", "PL", 7, A.arith_shift_right)
         ts("T8", "K7", 8.0, A.mult, 8.0, A.add)
         tt("P2", "T8", "PL", A.add)
         cp("P2U", "P2")
         cp("W2@P2U", "ONES")
         scan("N2", "W2:0:2720:2", "W2:1:2720:2", -160.0, A.add, A.add)
+        if again:
+            iota("W2", [[0, 2736]])
         scan("IX", "N2:3:1360:4", "MB", 0.0, A.min, A.max)
         ts("IXU", "IX:16:340:17", 159.0, A.add, 0.0, A.max)
         cp("MN", "O3@IXU")
@@ -332,12 +334,15 @@ def rank_program(g, core, T, topo):
         ts("CI", "PL", 3, A.arith_shift_right)
         cp("COFF", "CI")
 
-    fill("OWD", 0.0)
-    order("KFA", True, consts_early, consts_late, lambda: None)
+    def early0():
+        fill("W", -160.0)
+        fill("OWD", 0.0)
+
+    order("KFA", True, 2576, early0, consts_late, lambda: None)
     names = ["KFA", "KFB"]
     for t in range(R):
         last = t == R - 1
-        lists()
+        lists(not last)
         qz = "Z%d" % t
         for b in range(4):
             act("GB%d" % b, "FH%d@MOFF" % b, F.Copy)
@@ -352,15 +357,28 @@ def rank_program(g, core, T, topo):
         g.remote_dma(T["sA%d" % t][:, 0:C], T["s" + qz][:, 0:C], T.sem[arr], T.sem.sent, pid, rid, m)
         cnt["sent"], cnt[arr] = cnt.get("sent", 0) + n, n
         mm("PS", "UR", 0, qz)
+        mm("PSB", "UR", 0, qz)
         tt("SM", "PS:0:320", "MASK", A.mult)
-        act("DD", "PS:0:320", F.Abs, bias="TNY", scale=1.01 * 2.0 ** -24)
+        act("DD", "PSB:0:320", F.Abs, bias="TNY", scale=1.01 * 2.0 ** -24)
         scan("SS", "RS", "SM", 0.0, A.mult, A.add)
         tt("DM", "DD", "MSKA", A.mult)
         tt("RA", "PS:0:320", "DM", A.subtract)
-        for b in range(4):
+        tt("NM", "RA:%d:320" % CS, "MASK:%d:320" % CS, A.mult)
+        scan("ND", "RS:%d:320" % CS, "NM", 0.0, A.mult, A.add)
+        for w in range(WS, 5):
+            for e in range(4):
+                a = 4 * w + e
+                s, ct, d = "SS:%d:%d" % (16 * a + 15, 16 * a + 16), "CT%d:%%d:%%d:4" % w, "ND:%d:%d" % (16 * a - CS + 15, 16 * a - CS + 16)
+                if a:
+                    act(ct % (e, 64 * a), "PSB:0:%d" % (16 * a), F.Sign, bias=s, scale=-1.0)
+                act(ct % (64 * a + e, 64 * a + 64), "RA:%d:%d" % (16 * a, 16 * a + 16), F.Sign, bias=d, scale=-1.0)
+                if a < 19:
+                    act(ct % (64 * a + 64 + e, 4 * C), "PSB:%d:320" % (16 * a + 16), F.Sign, bias=d, scale=-1.0)
+            act("CT%d" % w, "CT%d" % w, F.Relu, scale=-1.0)
+        for b in range(2):
             act("FF%d" % b, "PF%d:0:320" % b, F.Copy)
         for w in range(5):
-            for e in range(4):
+            for e in range(4 if w < WS else 0):
                 a = 4 * w + e
                 s, ct = "SS:%d:%d" % (16 * a + 15, 16 * a + 16), "CT%d:%%d:%%d:4" % w
                 if a:
@@ -375,10 +393,11 @@ def rank_program(g, core, T, topo):
         tt(new, "STEP@COFF", old, A.add)
 
         def deal(t=t, arr=arr):
+            banks = ("PF0", "PF1", "PS", "PSB")
             for b in range(4):
-                mm("PF%d" % b, "L", P * b, "A%d" % t, extra=[(arr, cnt[arr])])
+                mm(banks[b], "L", P * b, "A%d" % t, extra=[(arr, cnt[arr])])
             for b in range(4):
-                act("HB%d" % b, "PF%d:1:320:2" % b, F.Copy, scale=0.03125)
+                act("HB%d" % b, banks[b] + ":1:320:2", F.Copy, scale=0.03125)
 
         def final(new=new):
             if last:
@@ -386,11 +405,15 @@ def rank_program(g, core, T, topo):
                 ts("PT1", "PT0", 2.0 ** -9, A.mult, -1.0, A.add)
                 quant("V", "VT")
 
-        order(new, not last, lambda: None, final, deal)
+        order(new, not last, (2896, 3216, NV)[t], lambda: None, final, deal)
         if last:
             dma("dpt", [("y", T.pt[:, :], T.PT1[0:P:16, :])], [], ["PT1"])
-        for b in range(4):
+        for b in (2, 3):
+            act("GB%d" % b, "HB%d@C2OFF" % b, F.Copy)
+        for b in (0, 1):
             tt("X:%d:1280:4" % b, "HB%d@C2OFF" % b, "FF%d" % b, A.add)
+        for b in (2, 3):
+            tt("X:%d:1280:4" % b, "GB%d" % b, "PF%d:0:320" % b, A.add)
         quant("X", "X")
         if not last:
             unpack()

@@ -4,7 +4,7 @@ C, P, R = 320, 128, 3
 NV = 3520
 NULL = 3528
 WW = 3936
-NS = 12
+NS = 11
 WS = 3
 CS = 64 * WS
 BIG = 4194304.0
@@ -25,41 +25,42 @@ def _t(n, d, parts, where="sbuf"):
     SCRATCH[n] = (where, [P, a], d)
 
 
-for _n, _w in (("E16", C), ("JR", C), ("T17", 340), ("E32", 640), ("TNY", 1), ("MASK", C), ("MSKA", C), ("RS", C), ("RS32", 640), ("MB0", 340),
-               ("MB", 340), ("KF0", C), ("KFA", C), ("KFB", C), ("KM", C), ("KS", C), ("SK", 352), ("S1", 340), ("S2", 340), ("GS", 640),
-               ("OWD", 336), ("O2", C), ("O3", C), ("IX", 340), ("MN", C), ("MM", C), ("MS", C), ("SM", C), ("SS", C), ("DD", C), ("DM", C),
-               ("RA", C), ("NM", C - CS), ("ND", C - CS), ("STEP", C), ("PT0", C), ("PT1", C), ("YB", C)):
+for _n, _w in (("E16", C), ("JR", C), ("T17", 340), ("E32", 640), ("TNY", 1), ("MASK", C), ("MSKA", C), ("RS", C), ("MB0", 340), ("MB", 340),
+               ("KF0", C), ("KFA", C), ("KFB", C), ("KM", C), ("KS", C), ("SK", 352), ("OWD", 336), ("O2", C), ("O3", C), ("IX", 340),
+               ("MM", C), ("MS", C), ("SM", C), ("SS", C), ("DD", C), ("DM", C), ("RA", C), ("NM", C - CS), ("ND", C - CS), ("STEP", C),
+               ("PT0", C), ("PT1", C), ("YB", C)):
     _b(_n, _w)
+_t("S12", "float32", [("S1", 340), ("S2", 340)])
 _t("CTAB", "float32", [("C16", 20), ("C1", 20), ("QP", 4), ("Q20", 4), ("ODD", 4), ("EVN", 4), ("NO", 4), ("NE", 4), ("DUMP", 20)])
-_t("FTAB", "float32", [("ACC", 20), ("RK", 20), ("O17", 20), ("DU", 20), ("DT", 20), ("OW", 20), ("PLF", 20), ("P2", 20)])
-_t("VSB", "float32", [("VS%d" % k, 160) for k in range(20 - NS)])
+_t("FTAB", "float32", [("ACC", 20), ("RK", 20), ("RKP", 20), ("O17", 20), ("DU", 20), ("DT", 20), ("OW", 20), ("P2", 20)])
+_t("VSB", "float16", [("VS%d" % k, 160) for k in range(20 - NS)])
+_b("GS", 640, "float16")
 _t("CTABI", "int32", [("QI", 4), ("QA", 4), ("QB", 4)])
-_t("ITAB", "int32", [("KI", 20), ("PI", 20), ("K1", 20), ("SI", 40), ("SH", 40), ("PL", 20), ("CI", 20), ("C2I", 20), ("K7", 20), ("T8", 20),
+_t("ITAB", "int32", [("KI", 20), ("PI", 20), ("K1", 20), ("SI", 40), ("SH", 40), ("PL", 20), ("CI", 20), ("C2I", 20), ("T8", 20),
                      ("MI", 20), ("MJ", 20), ("NJ", 20)])
 _t("UTAB", "uint16", [("OQ", 40)] + [(k, 20) for k in ("PERM", "RU", "RP", "OWU", "COFF", "C2OFF", "P2U", "IXU", "MOFF", "NOFF")])
 _b("UI", 8, "int32")
 _b("PR", C, "int32")
 _b("UL", 8, "uint16")
 for _n, _w in (("ZER", 512), ("ONE", 512), ("OB1", 512), ("OB2", 512), ("CDF", C), ("ONES", C), ("UT", 512), ("VT", 512), ("X", 4 * C),
-               ("Z", 4 * C), ("W", WW), ("CC", NV), ("D", 3536), ("G", 640), ("GT", 640), ("W2", 2736), ("N2", 1360)):
+               ("Z", 4 * C), ("W", WW), ("CC", NV), ("D", 3536), ("G", 640), ("GT", 640), ("W2", 2736), ("N2", 1360), ("RS32", 640)):
     _b(_n, _w, "bfloat16")
 _t("JUNK", "bfloat16", [("JUNK%d" % k, C) for k in range(NS)])
 _t("CMPB", "bfloat16", [("CMP%d" % k, C) for k in range(20 - NS)])
 _t("EBB", "bfloat16", [("EB%d" % k, 512) for k in range(4)])
-for _n, _w in (("FH", C), ("FF", C), ("GB", C), ("HB", 160)):
+for _n, _w in (("FH", C), ("GB", C), ("HB", 160)):
     _t(_n + "B", "bfloat16", [("%s%d" % (_n, k), _w) for k in range(4)])
 _t("CTB", "bfloat16", [("CT%d" % k, 4 * C) for k in range(5)])
 _t("PFB", "float32", [("PF%d" % k, 512) for k in range(4)], "psum")
-_b("PS", 512, "float32", "psum")
-_b("PSB", 512, "float32", "psum")
-_b("PK", 512, "float32", "psum")
+for _n in ("PS", "PSB", "PK", "PH"):
+    _b(_n, 512, "float32", "psum")
 for _n, _w in [("OB", P), ("U", P), ("UR", P), ("V", P), ("L", 512), ("X", C)] + [("%s%d" % (z, k), C) for k in range(R) for z in "ZA"]:
     _b("q" + _n, _w, "float8_e4m3fn_x4")
     _b("s" + _n, _w, "uint8")
 for _n, _d in (("q", "float8_e4m3fn_x4"), ("s", "uint8")):
     _t(_n + "EB", _d, [("%sE%d" % (_n, k), P) for k in range(4)])
     _t(_n + "CB", _d, [("%sC%d" % (_n, k), C) for k in range(5)])
-PSUM = ["PF0", "PF1", "PF2", "PF3", "PS", "PSB", "PK"]
+PSUM = ["PF0", "PF1", "PF2", "PF3", "PS", "PSB", "PK", "PH"]
 
 SEMAPHORES = ["cv", "cs", "ct", "cg", "dp", "dx", "du", "dv", "dw", "dd", "dout", "dpt", "dy", "sent"] + ["arr%d" % k for k in range(R)]
 
@@ -264,12 +265,8 @@ def rank_program(g, core, T, topo):
             ts("CMP%d" % k, kf, "KS:%d:%d" % (16 * c + 15, 16 * c + 16), A.is_lt)
             if k:
                 half(k - 1)
-        cp("KI", "KS:15:320:16")
-        half(n - 1)
-        ts("PI", "KI", 9, A.arith_shift_right)
         early()
-        ts("OQ:0:40:2", "PI", "EVN:0:1", A.mult, "NO:0:1", A.add)
-        ts("OQ:1:40:2", "PI", "ODD:0:1", A.mult, "NE:0:1", A.add)
+        half(n - 1)
         op("v", lambda: V.tensor_copy(ap("RK:%d:20" % NS), T.VSB[:, 159:160 * n:160]), ["RK:%d:20" % NS], ["VS%d" % k for k in range(n)])
         ts("RK:0:%d" % NS, "ACC:0:%d" % NS, 319.0, A.add, 0.5, A.mult)
         ts("K1", "RK", 0.0625, A.mult, 0.53125, A.add)
@@ -279,8 +276,7 @@ def rank_program(g, core, T, topo):
         cp("SK:17:340:17", "SK:18:341:17")
         scan("S1", "SK:0:340", "MB", 0.0, A.min, A.max)
         scan("S2", "SK:1:341", "MB", 0.0, A.min, A.max)
-        cp("SI:0:20", "S1:16:340:17")
-        cp("SI:20:40", "S2:16:340:17")
+        op("v", lambda: V.tensor_copy(ap("SI"), T.S12[:, 16:680:17]), ["SI"], ["S1", "S2"])
         ts("SH", "SI", 9, A.arith_shift_right)
         tt("DU", "SH:0:20", "SH:20:40", A.is_equal)
         tt("DT", "DU", "DUMP", A.mult)
@@ -296,9 +292,15 @@ def rank_program(g, core, T, topo):
                 moves.append((T.D[h:16 * h:16, 1:nv], T.CC[16 * h + 8:16 * h + 8 + h, 0:nv - 1]))
         dma("dd", [("ys"[k % 2], o, i) for k, (o, i) in enumerate(moves)], ["D"], ["CC"])
         scalar_tail()
+        cp("KI", "KS:15:320:16")
+        ts("RKP", "RK", 1120.0, A.add)
+        ts("PI", "KI", 9, A.arith_shift_right)
         if joined:
             iota("W", [[0, WW]], -160)
             cp("RU", "RK")
+        ts("OQ:0:40:2", "PI", "EVN:0:1", A.mult, "NO:0:1", A.add)
+        ts("OQ:1:40:2", "PI", "ODD:0:1", A.mult, "NE:0:1", A.add)
+        if joined:
             cp("OWD@RU", "JR")
             cp("OWD:320:321", "OWD:319:320")
             ts("O2", "OWD:0:320", 512.0, A.mult)
@@ -307,42 +309,42 @@ def rank_program(g, core, T, topo):
         cp("G", "D@OQ")
         op("v", lambda: V.transpose(ap("GT"), ap("G")), ["GT"], ["G"])
         scan("GS", "RS32", "GT", 0.0, A.mult, A.add)
-        tt("PLF", "GS:31:640:32", "RK", A.add)
-        ts("PL", "PLF", 1120.0, A.add)
+        tt("PL", "GS:31:640:32", "RKP", A.add)
         ts("C2I", "PL", 4, A.arith_shift_right)
         cp("C2OFF", "C2I")
 
-    def lists(again):
-        ts("K7", "PL", 7, A.arith_shift_right)
-        ts("T8", "K7", 8.0, A.mult, 8.0, A.add)
+    def lists1(again):
+        ts("T8", "PL", 4, A.arith_shift_right, 0xFFF8, A.bitwise_and)
+        ts("CI", "PL", 3, A.arith_shift_right)
         tt("P2", "T8", "PL", A.add)
-        cp("P2U", "P2")
+        cp("COFF", "CI")
+        ts("P2U", "P2", 8.0, A.add)
         cp("W2@P2U", "ONES")
         scan("N2", "W2:0:2720:2", "W2:1:2720:2", -160.0, A.add, A.add)
         if again:
             iota("W2", [[0, 2736]])
+
+    def lists2():
         scan("IX", "N2:3:1360:4", "MB", 0.0, A.min, A.max)
         ts("IXU", "IX:16:340:17", 159.0, A.add, 0.0, A.max)
-        cp("MN", "O3@IXU")
-        tt("MM", "MN", "MASK", A.mult)
+        tt("MM", "O3@IXU", "MASK", A.mult)
         scan("MS", "RS", "MM", 0.0, A.mult, A.add)
         cp("MI", "MS:15:320:16")
         ts("MJ", "MI", 9, A.arith_shift_right)
         ts("NJ", "MI", 511, A.bitwise_and)
         cp("MOFF", "MJ")
         cp("NOFF", "NJ")
-        ts("CI", "PL", 3, A.arith_shift_right)
-        cp("COFF", "CI")
 
     def early0():
         fill("W", -160.0)
         fill("OWD", 0.0)
 
     order("KFA", True, 2576, early0, consts_late, lambda: None)
+    lists1(True)
     names = ["KFA", "KFB"]
     for t in range(R):
         last = t == R - 1
-        lists(not last)
+        lists2()
         qz = "Z%d" % t
         for b in range(4):
             act("GB%d" % b, "FH%d@MOFF" % b, F.Copy)
@@ -375,8 +377,6 @@ def rank_program(g, core, T, topo):
                 if a < 19:
                     act(ct % (64 * a + 64 + e, 4 * C), "PSB:%d:320" % (16 * a + 16), F.Sign, bias=d, scale=-1.0)
             act("CT%d" % w, "CT%d" % w, F.Relu, scale=-1.0)
-        for b in range(2):
-            act("FF%d" % b, "PF%d:0:320" % b, F.Copy)
         for w in range(5):
             for e in range(4 if w < WS else 0):
                 a = 4 * w + e
@@ -393,7 +393,7 @@ def rank_program(g, core, T, topo):
         tt(new, "STEP@COFF", old, A.add)
 
         def deal(t=t, arr=arr):
-            banks = ("PF0", "PF1", "PS", "PSB")
+            banks = ("PH", "PS", "PSB", "PK")
             for b in range(4):
                 mm(banks[b], "L", P * b, "A%d" % t, extra=[(arr, cnt[arr])])
             for b in range(4):
@@ -408,11 +408,11 @@ def rank_program(g, core, T, topo):
         order(new, not last, (2896, 3216, NV)[t], lambda: None, final, deal)
         if last:
             dma("dpt", [("y", T.pt[:, :], T.PT1[0:P:16, :])], [], ["PT1"])
-        for b in (2, 3):
+        for b in range(4):
             act("GB%d" % b, "HB%d@C2OFF" % b, F.Copy)
-        for b in (0, 1):
-            tt("X:%d:1280:4" % b, "HB%d@C2OFF" % b, "FF%d" % b, A.add)
-        for b in (2, 3):
+        if not last:
+            lists1(t + 1 < R - 1)
+        for b in range(4):
             tt("X:%d:1280:4" % b, "GB%d" % b, "PF%d:0:320" % b, A.add)
         quant("X", "X")
         if not last:

@@ -25,25 +25,24 @@ def _t(n, d, parts, where="sbuf"):
     SCRATCH[n] = (where, [P, a], d)
 
 
-for _n, _w in (("E16", C), ("JR", C), ("T17", 340), ("E32", 640), ("TNY", 1), ("MASK", C), ("MSKA", C), ("RS", C), ("MB0", 340), ("MB", 340),
-               ("KF0", C), ("KFA", C), ("KFB", C), ("KM", C), ("KS", C), ("SK", 352), ("OWD", 336), ("O2", C), ("O3", C), ("IX", 340),
-               ("MM", C), ("MS", C), ("SM", C), ("SS", C), ("DD", C), ("DM", C), ("RA", C), ("NM", C - CS), ("ND", C - CS), ("STEP", C),
+for _n, _w in (("E16", C), ("JR", C), ("E32", 640), ("TNY", 1), ("MASK", C), ("MSKA", C), ("RS", C), ("MB0", C), ("MB", C),
+               ("KF0", C), ("KFA", C), ("KFB", C), ("KM", C), ("KS", C), ("S1", C), ("S2", C), ("OWD", 336), ("O2", C), ("O3", C), ("IX", C),
+               ("MM", C), ("MS", C), ("SM", C), ("SS", C), ("DD", C), ("DM", C), ("RA", C), ("NA", 20 - 4 * WS), ("ND", 20 - 4 * WS), ("STEP", C),
                ("PT0", C), ("PT1", C), ("YB", C)):
     _b(_n, _w)
-_t("S12", "float32", [("S1", 340), ("S2", 340)])
+_t("SKB", "float32", [("SK", C), ("SKE", 16)])
 _t("CTAB", "float32", [("C16", 20), ("C1", 20), ("QP", 4), ("Q20", 4), ("ODD", 4), ("EVN", 4), ("NO", 4), ("NE", 4), ("DUMP", 20)])
-_t("FTAB", "float32", [("ACC", 20), ("RK", 20), ("RKP", 20), ("O17", 20), ("DU", 20), ("DT", 20), ("OW", 20), ("P2", 20)])
+_t("FTAB", "float32", [("ACC", 20), ("RKP", 20), ("DU", 20), ("DT", 20), ("OW", 20), ("IXM", 20)])
 _t("VSB", "float16", [("VS%d" % k, 160) for k in range(20 - NS)])
 _b("GS", 640, "float16")
 _t("CTABI", "int32", [("QI", 4), ("QA", 4), ("QB", 4)])
-_t("ITAB", "int32", [("KI", 20), ("PI", 20), ("K1", 20), ("SI", 40), ("SH", 40), ("PL", 20), ("CI", 20), ("C2I", 20), ("T8", 20),
-                     ("MI", 20), ("MJ", 20), ("NJ", 20)])
-_t("UTAB", "uint16", [("OQ", 40)] + [(k, 20) for k in ("PERM", "RU", "RP", "OWU", "COFF", "C2OFF", "P2U", "IXU", "MOFF", "NOFF")])
+_t("ITAB", "int32", [("KI", 20), ("PI", 20), ("SI", 40), ("SH", 40), ("PL", 20), ("CI", 20), ("C2I", 20), ("MI", 20), ("MJ", 20), ("NJ", 20)])
+_t("UTAB", "uint16", [("OQ", 40)] + [(k, 20) for k in ("PERM", "RP", "OWU", "COFF", "C2OFF", "P2U", "IXU", "MOFF", "NOFF")])
 _b("UI", 8, "int32")
 _b("PR", C, "int32")
 _b("UL", 8, "uint16")
 for _n, _w in (("ZER", 512), ("ONE", 512), ("OB1", 512), ("OB2", 512), ("CDF", C), ("ONES", C), ("UT", 512), ("VT", 512), ("X", 4 * C),
-               ("Z", 4 * C), ("W", WW), ("CC", NV), ("D", 3536), ("G", 640), ("GT", 640), ("W2", 2736), ("N2", 1360), ("RS32", 640)):
+               ("Z", 4 * C), ("W", WW), ("CC", NV), ("D", 3536), ("G", 640), ("GT", 640), ("W2", 8 * C), ("N2", 4 * C), ("RS32", 640)):
     _b(_n, _w, "bfloat16")
 _t("JUNK", "bfloat16", [("JUNK%d" % k, C) for k in range(NS)])
 _t("CMPB", "bfloat16", [("CMP%d" % k, C) for k in range(20 - NS)])
@@ -62,7 +61,7 @@ for _n, _d in (("q", "float8_e4m3fn_x4"), ("s", "uint8")):
     _t(_n + "CB", _d, [("%sC%d" % (_n, k), C) for k in range(5)])
 PSUM = ["PF0", "PF1", "PF2", "PF3", "PS", "PSB", "PK", "PH"]
 
-SEMAPHORES = ["cv", "cs", "ct", "cg", "dp", "dx", "du", "dv", "dw", "dd", "dout", "dpt", "dy", "sent"] + ["arr%d" % k for k in range(R)]
+SEMAPHORES = ["cv", "cs", "ct", "cg", "dp", "dx", "du", "dv", "dw", "dz", "dd", "de", "dout", "dpt", "dy", "sent"] + ["arr%d" % k for k in range(R)]
 
 
 def region(s):
@@ -158,7 +157,8 @@ def rank_program(g, core, T, topo):
         op("v", lambda: V.tensor_copy(ap(o), ap(i)), [o], [i])
 
     def scan(o, a, b, init, op0, op1):
-        op("v", lambda: V.tensor_tensor_scan(ap(o), ap(a), ap(b), init, op0, op1), [o], [a, b])
+        first = isinstance(init, str)
+        op("v", lambda: V.tensor_tensor_scan(ap(o), ap(a), ap(b), ap(init) if first else init, op0, op1), [o], [a, b] + ([init] if first else []))
 
     def fill(n, c):
         op("v", lambda: V.memset(ap(n), c), [n], [])
@@ -191,16 +191,19 @@ def rank_program(g, core, T, topo):
     dma("dp", [("ys"[k % 2], T.PR[k:P:16, :], T.p[:, :]) for k in range(16)], ["PR"], [])
     dma("dx", [("y", T.X[:, :], T.x[:, :])], ["X"], [])
     dma("du", [("y", T.UT[:, :], T.u[:, :])], ["UT"], [])
-    dma("dw", [("y", T.qL[:, 0:512].bitcast(dt.uint8), T.wc[:, :]), ("y", T.sL[:, 0:512], T.ws[:, :])], ["qL", "sL"], [])
-    dma("dv", [("y", T.VT[:, :], T.v[:, :])], ["VT"], [])
 
     iota("QI:0:2", [[0, 2]], 0, 1)
     iota("C1", [[1, 20]])
     iota("E16", [[0, 20], [1, 16]])
     iota("JR", [[1, C]])
-    iota("T17", [[0, 20], [1, 17]])
     iota("C16", [[16, 20]])
-    fill("D", 0.0)
+    iota("E32", [[0, 20], [1, 32]])
+    iota("W", [[0, WW]], -160)
+    fill("ZER", 0.0)
+    fill("ONE", 1.0)
+    dma("dz", [("y", T.D[:, a:min(a + 512, 3536)], T.ZER[:, 0:min(512, 3536 - a)]) for a in range(0, 3536, 512)], ["D"], ["ZER"])
+    dma("dw", [("y", T.qL[:, 0:512].bitcast(dt.uint8), T.wc[:, :]), ("y", T.sL[:, 0:512], T.ws[:, :])], ["qL", "sL"], [])
+    dma("dv", [("y", T.VT[:, :], T.v[:, :])], ["VT"], [])
     ts("QA:0:2", "QI:0:2", 15, A.bitwise_and)
     ts("QB:0:2", "QI:0:2", 4, A.arith_shift_right, 1, A.bitwise_and)
     cp("QP:0:1", "QA:0:1")
@@ -212,20 +215,19 @@ def rank_program(g, core, T, topo):
     ts("NE:0:1", "EVN:0:1", float(NULL), A.mult)
     ts("MASK", "E16", "QP:0:1", A.is_equal)
     ts("RS", "E16", 0.0, A.is_gt)
-    ts("MB0", "T17", "QP:0:1", A.is_le)
+    ts("MB0", "E16", "QP:0:1", A.is_lt)
     ts("CDF", "JR", -159.0, A.add)
-    fill("SK", 3600.0 * 512.0)
     ts("MB", "MB0", 2.0 * BIG, A.mult, -BIG, A.add)
     ts("DUMP", "C16", "QP:0:1", A.add, 3600.0, A.add)
-    fill("ZER", 0.0)
-    fill("ONE", 1.0)
+    fill("SKE", 3600.0 * 512.0)
+    fill("ONES", 1.0)
+    act("RS32", "E32", F.Sign)
     for b in range(4):
         sel("EB%d" % b, "ZER", [[1, 512]], A.not_equal, 1.0, -b, -4)
-    iota("E32", [[0, 20], [1, 32]])
+    iota("W2", [[0, 8 * C]])
     iota("UI", [[16, 8]])
     sel("OB1", "ONE", [[-16, 8], [0, 64]], A.is_ge, 0.0, 0, 1)
     sel("OB2", "OB1", [[16, 8], [0, 64]], A.is_ge, 0.0, 15, -1)
-    iota("W2", [[0, 2736]])
     cp("KF0", "PR@PERM")
     ts("KFB", "KF0", 512.0, A.mult, 512.0, A.add)
     tt("KFA", "KFB", "JR", A.add)
@@ -236,25 +238,34 @@ def rank_program(g, core, T, topo):
         for b in range(4):
             act("FH%d" % b, "PF%d:0:320" % b, F.Copy, scale=0.5)
 
-    def consts_late():
+    def first_tiles():
         for b in range(4):
             quant("E%d" % b, "EB%d" % b)
         quant("X", "X")
         unpack()
-        ts("RS32", "E32", 0.0, A.is_gt)
+
+    def sides():
         cp("UL", "UI")
         quant("U", "UT")
+        quant("OB", "OB2")
         op("v", lambda: V.tensor_copy(T.qUR[:, 0:P].bitcast(dt.uint32), T.qU[:, 0:P].bitcast(dt.uint32).indirect(T.UL[:, 0:8])), ["qUR"], ["qU", "UL"])
         cp("sUR", "sU@UL")
-        quant("OB", "OB2")
-        fill("ONES", 1.0)
         fill("TNY", 2.0 ** -126)
         ts("MSKA", "E16", "QP:0:1", A.is_le)
 
     def half(k):
         scan("VS%d" % k, "CMP%d:0:160" % k, "CMP%d:160:320" % k, 0.0, A.add, A.add)
 
-    def order(kf, joined, nv, early, during, scalar_tail):
+    def spread(sem, a, b):
+        moves = []
+        for h in range(8):
+            if h < 7:
+                moves.append((T.D[16 * (h + 1) + h:P:16, a:b], T.CC[16 * h:16 * h + 7 - h, a:b]))
+            if h:
+                moves.append((T.D[h:16 * h:16, a + 1:b + 1], T.CC[16 * h + 8:16 * h + 8 + h, a:b]))
+        dma(sem, [("ys"[k % 2], o, i) for k, (o, i) in enumerate(moves)], ["D:%d:%d" % (a, b)], ["CC:%d:%d" % (a, b)])
+
+    def order(kf, joined, nv, during, scalar_tail):
         tt("KM", kf, "MASK", A.mult)
         scan("KS", "RS", "KM", 0.0, A.mult, A.add)
         for c in range(NS):
@@ -265,43 +276,36 @@ def rank_program(g, core, T, topo):
             ts("CMP%d" % k, kf, "KS:%d:%d" % (16 * c + 15, 16 * c + 16), A.is_lt)
             if k:
                 half(k - 1)
-        early()
         half(n - 1)
-        op("v", lambda: V.tensor_copy(ap("RK:%d:20" % NS), T.VSB[:, 159:160 * n:160]), ["RK:%d:20" % NS], ["VS%d" % k for k in range(n)])
-        ts("RK:0:%d" % NS, "ACC:0:%d" % NS, 319.0, A.add, 0.5, A.mult)
-        ts("K1", "RK", 0.0625, A.mult, 0.53125, A.add)
-        tt("O17", "RK", "K1", A.add)
-        cp("RP", "O17")
+        ts("RP:0:%d" % NS, "ACC:0:%d" % NS, 319.0, A.add, 0.5, A.mult)
+        op("v", lambda: V.tensor_copy(ap("RP:%d:20" % NS), T.VSB[:, 159:160 * n:160]), ["RP:%d:20" % NS], ["VS%d" % k for k in range(n)])
         cp("SK@RP", kf)
-        cp("SK:17:340:17", "SK:18:341:17")
-        scan("S1", "SK:0:340", "MB", 0.0, A.min, A.max)
-        scan("S2", "SK:1:341", "MB", 0.0, A.min, A.max)
-        op("v", lambda: V.tensor_copy(ap("SI"), T.S12[:, 16:680:17]), ["SI"], ["S1", "S2"])
+        scan("S1", "SK", "MB", 0.0, A.min, A.max)
+        op("v", lambda: V.tensor_tensor_scan(ap("S2"), T.SKB[:, 1:C + 1], ap("MB"), 0.0, A.min, A.max), ["S2"], ["SK", "SKE", "MB"])
+        tt("SI:0:20", "S1:15:320:16", "SK:0:320:16", A.max)
+        tt("SI:20:40", "S2:15:320:16", "SK:1:320:16", A.max)
         ts("SH", "SI", 9, A.arith_shift_right)
         tt("DU", "SH:0:20", "SH:20:40", A.is_equal)
         tt("DT", "DU", "DUMP", A.mult)
         tt("OW", "DT", "SH:0:20", A.max)
         cp("OWU", "OW")
         cp("W@OWU", "CDF")
-        scan("CC:0:%d" % nv, "W:0:%d" % nv, "W:0:%d" % nv, -160.0, A.max, A.max)
-        moves = []
-        for h in range(8):
-            if h < 7:
-                moves.append((T.D[16 * (h + 1) + h:P:16, 0:nv], T.CC[16 * h:16 * h + 7 - h, 0:nv]))
-            if h:
-                moves.append((T.D[h:16 * h:16, 1:nv], T.CC[16 * h + 8:16 * h + 8 + h, 0:nv - 1]))
-        dma("dd", [("ys"[k % 2], o, i) for k, (o, i) in enumerate(moves)], ["D"], ["CC"])
+        h = nv // 2
+        lo, hi = "0:%d" % h, "%d:%d" % (h, nv)
+        scan("CC:" + lo, "W:" + lo, "W:" + lo, -160.0, A.max, A.max)
+        spread("dd", 0, h)
+        scan("CC:" + hi, "W:" + hi, "W:" + hi, "CC:%d:%d" % (h - 1, h), A.max, A.max)
+        spread("de", h, nv)
         scalar_tail()
         cp("KI", "KS:15:320:16")
-        ts("RKP", "RK", 1120.0, A.add)
+        ts("RKP", "RP", 1120.0, A.add)
         ts("PI", "KI", 9, A.arith_shift_right)
         if joined:
             iota("W", [[0, WW]], -160)
-            cp("RU", "RK")
+            cp("OWD@RP", "JR")
         ts("OQ:0:40:2", "PI", "EVN:0:1", A.mult, "NO:0:1", A.add)
         ts("OQ:1:40:2", "PI", "ODD:0:1", A.mult, "NE:0:1", A.add)
         if joined:
-            cp("OWD@RU", "JR")
             cp("OWD:320:321", "OWD:319:320")
             ts("O2", "OWD:0:320", 512.0, A.mult)
             tt("O3", "O2", "OWD:1:321", A.add)
@@ -314,32 +318,27 @@ def rank_program(g, core, T, topo):
         cp("C2OFF", "C2I")
 
     def lists1(again):
-        ts("T8", "PL", 4, A.arith_shift_right, 0xFFF8, A.bitwise_and)
+        cp("P2U", "PL")
         ts("CI", "PL", 3, A.arith_shift_right)
-        tt("P2", "T8", "PL", A.add)
-        cp("COFF", "CI")
-        ts("P2U", "P2", 8.0, A.add)
         cp("W2@P2U", "ONES")
-        scan("N2", "W2:0:2720:2", "W2:1:2720:2", -160.0, A.add, A.add)
+        cp("COFF", "CI")
+        scan("N2", "W2:0:2560:2", "W2:1:2560:2", -160.0, A.add, A.add)
         if again:
-            iota("W2", [[0, 2736]])
+            iota("W2", [[0, 8 * C]])
 
     def lists2():
-        scan("IX", "N2:3:1360:4", "MB", 0.0, A.min, A.max)
-        ts("IXU", "IX:16:340:17", 159.0, A.add, 0.0, A.max)
+        scan("IX", "N2:3:1280:4", "MB", 0.0, A.min, A.max)
+        tt("IXM", "IX:15:320:16", "N2:3:1280:64", A.max)
+        ts("IXU", "IXM", 159.0, A.add, 0.0, A.max)
         tt("MM", "O3@IXU", "MASK", A.mult)
         scan("MS", "RS", "MM", 0.0, A.mult, A.add)
+        ts("MJ", "MS:15:320:16", 2.0 ** -9, A.mult, -0.3125, A.add)
         cp("MI", "MS:15:320:16")
-        ts("MJ", "MI", 9, A.arith_shift_right)
-        ts("NJ", "MI", 511, A.bitwise_and)
         cp("MOFF", "MJ")
+        ts("NJ", "MI", 511, A.bitwise_and)
         cp("NOFF", "NJ")
 
-    def early0():
-        fill("W", -160.0)
-        fill("OWD", 0.0)
-
-    order("KFA", True, 2576, early0, consts_late, lambda: None)
+    order("KFA", True, 2576, first_tiles, lambda: None)
     lists1(True)
     names = ["KFA", "KFB"]
     for t in range(R):
@@ -348,6 +347,8 @@ def rank_program(g, core, T, topo):
         qz = "Z%d" % t
         for b in range(4):
             act("GB%d" % b, "FH%d@MOFF" % b, F.Copy)
+        if t == 0:
+            sides()
         for b in range(4):
             tt("Z:%d:1280:4" % b, "FH%d@NOFF" % b, "GB%d" % b, A.add)
         quant(qz, "Z")
@@ -364,13 +365,14 @@ def rank_program(g, core, T, topo):
         act("DD", "PSB:0:320", F.Abs, bias="TNY", scale=1.01 * 2.0 ** -24)
         scan("SS", "RS", "SM", 0.0, A.mult, A.add)
         tt("DM", "DD", "MSKA", A.mult)
+        keys = "SS:%d:320:16" % (CS + 15)
+        act("NA", keys, F.Abs, bias="TNY", scale=1.01 * 2.0 ** -24)
         tt("RA", "PS:0:320", "DM", A.subtract)
-        tt("NM", "RA:%d:320" % CS, "MASK:%d:320" % CS, A.mult)
-        scan("ND", "RS:%d:320" % CS, "NM", 0.0, A.mult, A.add)
+        tt("ND", keys, "NA", A.subtract)
         for w in range(WS, 5):
             for e in range(4):
                 a = 4 * w + e
-                s, ct, d = "SS:%d:%d" % (16 * a + 15, 16 * a + 16), "CT%d:%%d:%%d:4" % w, "ND:%d:%d" % (16 * a - CS + 15, 16 * a - CS + 16)
+                s, ct, d = "SS:%d:%d" % (16 * a + 15, 16 * a + 16), "CT%d:%%d:%%d:4" % w, "ND:%d:%d" % (a - 4 * WS, a - 4 * WS + 1)
                 if a:
                     act(ct % (e, 64 * a), "PSB:0:%d" % (16 * a), F.Sign, bias=s, scale=-1.0)
                 act(ct % (64 * a + e, 64 * a + 64), "RA:%d:%d" % (16 * a, 16 * a + 16), F.Sign, bias=d, scale=-1.0)
@@ -405,11 +407,14 @@ def rank_program(g, core, T, topo):
                 ts("PT1", "PT0", 2.0 ** -9, A.mult, -1.0, A.add)
                 quant("V", "VT")
 
-        order(new, not last, (2896, 3216, NV)[t], lambda: None, final, deal)
+        order(new, not last, (2896, 3216, NV)[t], final, deal)
         if last:
             dma("dpt", [("y", T.pt[:, :], T.PT1[0:P:16, :])], [], ["PT1"])
         for b in range(4):
-            act("GB%d" % b, "HB%d@C2OFF" % b, F.Copy)
+            if last and b > 1:
+                cp("GB%d" % b, "HB%d@C2OFF" % b)
+            else:
+                act("GB%d" % b, "HB%d@C2OFF" % b, F.Copy)
         if not last:
             lists1(t + 1 < R - 1)
         for b in range(4):

from concourse.mybir import dt, AluOpType as A, ActivationFunctionType as F

C, P, R = 320, 128, 3
NV = 3520
NULL = 3528
WW = 3936
NS = 11
WS = 3
CS = 64 * WS
BIG = 4194304.0

SCRATCH, AT = {}, {}


def _b(n, w, d="float32", where="sbuf"):
    SCRATCH[n] = (where, [P, w], d)
    AT[n] = (n, 0, w)


def _t(n, d, parts, where="sbuf"):
    a = 0
    for k, w in parts:
        AT[k] = (n, a, w)
        a += w
    SCRATCH[n] = (where, [P, a], d)


for _n, _w in (("E16", C), ("JR", C), ("E32", 640), ("TNY", 1), ("MASK", C), ("MSKA", C), ("RS", C), ("MB0", C), ("MB", C),
               ("KF0", C), ("KFA", C), ("KFB", C), ("KM", C), ("KS", C), ("S1", C), ("S2", C), ("OWD", 336), ("O2", C), ("O3", C), ("IX", C),
               ("MM", C), ("MS", C), ("SM", C), ("SS", C), ("DD", C), ("DM", C), ("RA", C), ("NA", 20 - 4 * WS), ("ND", 20 - 4 * WS), ("STEP", C),
               ("PT0", C), ("PT1", C), ("YB", C)):
    _b(_n, _w)
_t("SKB", "float32", [("SK", C), ("SKE", 16)])
_t("CTAB", "float32", [("C16", 20), ("C1", 20), ("QP", 4), ("Q20", 4), ("ODD", 4), ("EVN", 4), ("NO", 4), ("NE", 4), ("DUMP", 20)])
_t("FTAB", "float32", [("ACC", 20), ("RKP", 20), ("DU", 20), ("DT", 20), ("OW", 20), ("IXM", 20)])
_t("VSB", "float16", [("VS%d" % k, 160) for k in range(20 - NS)])
_b("GS", 640, "float16")
_t("CTABI", "int32", [("QI", 4), ("QA", 4), ("QB", 4)])
_t("ITAB", "int32", [("KI", 20), ("PI", 20), ("SI", 40), ("SH", 40), ("PL", 20), ("CI", 20), ("C2I", 20), ("MI", 20), ("MJ", 20), ("NJ", 20)])
_t("UTAB", "uint16", [("OQ", 40)] + [(k, 20) for k in ("PERM", "RP", "OWU", "COFF", "C2OFF", "P2U", "IXU", "MOFF", "NOFF")])
_b("UI", 8, "int32")
_b("PR", C, "int32")
_b("UL", 8, "uint16")
for _n, _w in (("ZER", 512), ("ONE", 512), ("OB1", 512), ("OB2", 512), ("CDF", C), ("ONES", C), ("UT", 512), ("VT", 512), ("X", 4 * C),
               ("Z", 4 * C), ("W", WW), ("CC", NV), ("D", 3536), ("G", 640), ("GT", 640), ("W2", 8 * C), ("N2", 4 * C), ("RS32", 640)):
    _b(_n, _w, "bfloat16")
_t("JUNK", "bfloat16", [("JUNK%d" % k, C) for k in range(NS)])
_t("CMPB", "bfloat16", [("CMP%d" % k, C) for k in range(20 - NS)])
_t("EBB", "bfloat16", [("EB%d" % k, 512) for k in range(4)])
for _n, _w in (("FH", C), ("GB", C), ("HB", 160)):
    _t(_n + "B", "bfloat16", [("%s%d" % (_n, k), _w) for k in range(4)])
_t("CTB", "bfloat16", [("CT%d" % k, 4 * C) for k in range(5)])
_t("PFB", "float32", [("PF%d" % k, 512) for k in range(4)], "psum")
for _n in ("PS", "PSB", "PK", "PH"):
    _b(_n, 512, "float32", "psum")
for _n, _w in [("OB", P), ("U", P), ("UR", P), ("V", P), ("L", 512), ("X", C)] + [("%s%d" % (z, k), C) for k in range(R) for z in "ZA"]:
    _b("q" + _n, _w, "float8_e4m3fn_x4")
    _b("s" + _n, _w, "uint8")
for _n, _d in (("q", "float8_e4m3fn_x4"), ("s", "uint8")):
    _t(_n + "EB", _d, [("%sE%d" % (_n, k), P) for k in range(4)])
    _t(_n + "CB", _d, [("%sC%d" % (_n, k), C) for k in range(5)])
PSUM = ["PF0", "PF1", "PF2", "PF3", "PS", "PSB", "PK", "PH"]

SEMAPHORES = ["cv", "cs", "ct", "cg", "dp", "dx", "du", "dv", "dw", "dz", "dd", "de", "dout", "dpt", "dy", "sent"] + ["arr%d" % k for k in range(R)]


def region(s):
    f = s.split("@")[0].split(":")
    if len(f) < 3 or "@" in s:
        return f[0], range(AT[f[0]][2])
    return f[0], range(int(f[1]), int(f[2]), int((f + [1])[3]))


def meet(a, b):
    if a[-1] < b[0] or b[-1] < a[0]:
        return False
    return a.step == 1 or b.step == 1 or a.step != b.step or (a[0] - b[0]) % a.step == 0


def rank_program(g, core, T, topo):
    rank = T.rank_of(core)
    if rank is None:
        return
    nxt = T.cores[(rank + 1) % len(T.cores)]
    V, S, TE = g.vector, g.scalar, g.tensor
    eng = {"v": V, "s": S, "t": TE, "g": g, "y": g.sync}
    cnt, seen, wr, rd = {}, {e: {} for e in eng}, {}, {}

    def ap(s):
        s, _x, by = s.partition("@")
        n, o, w = AT[s.split(":")[0]]
        r = region(s)[1]
        a, e = o + r.start, o + r.stop
        v = T[n][:, a:e:r.step] if r.step > 1 else T[n][:, a:e]
        return v.indirect(ap(by)) if by else v

    def wait(e, deps):
        most = {}
        for s, n in deps:
            most[s] = max(most.get(s, 0), n)
        for s, n in most.items():
            if seen[e].get(s, 0) < n:
                eng[e].wait_ge(T.sem[s], n)
                seen[e][s] = n

    def deps_of(outs, ins, own):
        d = []
        for k, r in ins:
            d += [x[1:] for x in wr.get(k, []) if meet(x[0], r)]
            if k in PSUM:
                d += [x[1:] for x in rd.get(k, []) if x[1] != own]
        for k, r in outs:
            for x in wr.get(k, []) + rd.get(k, []):
                if (meet(x[0], r) or k in PSUM) and not (own == "ct" and x[1] == own):
                    d.append(x[1:])
        return d

    def note(outs, ins, sem, n):
        for k, r in ins:
            rd[k] = [x for x in rd.get(k, []) if x[1] != sem or x[0] != r] + [(r, sem, n)]
        for k, r in outs:
            whole = len(r) == AT[k][2] or k in PSUM
            wr[k] = ([] if whole else [x for x in wr.get(k, []) if x[0] != r]) + [(r, sem, n)]
            if whole:
                rd[k] = [x for x in rd.get(k, []) if x[2] == n and x[1] == sem]

    def op(e, call, outs, ins, extra=()):
        own = "c" + e
        lists = [s.split("@")[1] for s in list(outs) + list(ins) if "@" in s]
        o, i = [region(s) for s in outs], [region(s) for s in list(ins) + lists]
        wait(e, deps_of(o, i, own) + list(extra))
        cnt[own] = cnt.get(own, 0) + 1
        call().then_inc(T.sem[own], 1)
        note(o, i, own, cnt[own])

    def dma(sem, moves, outs, ins):
        o, i = [region(s) for s in outs], [region(s) for s in ins]
        d = deps_of(o, i, "")
        for q, to, fr in moves:
            wait(q, d)
            eng[q].dma_start(to, fr).then_inc(T.sem[sem], 16)
            cnt[sem] = cnt.get(sem, 0) + 16
        note(o, i, sem, cnt[sem])

    def ts(o, i, s1, op0, s2=None, op1=None):
        a1, a2 = [ap(s) if isinstance(s, str) else s for s in (s1, s2)]
        names = [i] + [s for s in (s1, s2) if isinstance(s, str)]
        if op1 is None:
            op("v", lambda: V.tensor_scalar(ap(o), ap(i), a1, None, op0), [o], names)
        else:
            op("v", lambda: V.tensor_scalar(ap(o), ap(i), a1, a2, op0, op1), [o], names)

    def tt(o, a, b, o2):
        op("v", lambda: V.tensor_tensor(ap(o), ap(a), ap(b), o2), [o], [a, b])

    def cp(o, i):
        op("v", lambda: V.tensor_copy(ap(o), ap(i)), [o], [i])

    def scan(o, a, b, init, op0, op1):
        first = isinstance(init, str)
        op("v", lambda: V.tensor_tensor_scan(ap(o), ap(a), ap(b), ap(init) if first else init, op0, op1), [o], [a, b] + ([init] if first else []))

    def fill(n, c):
        op("v", lambda: V.memset(ap(n), c), [n], [])

    def quant(q, t):
        op("v", lambda: V.quantize_mx(ap("q" + q), ap("s" + q), ap(t)), ["q" + q, "s" + q], [t])

    def mm(ps, a, a0, b, start=True, stop=True, extra=()):
        r = ":%d:%d" % (a0, a0 + P)
        i = ["q" + a + r, "s" + a + r, "q" + b, "s" + b]
        op("t", lambda: TE.matmul_mx(ap(ps + ":0:320"), ap(i[0]), ap(i[1]), ap(i[2]), ap(i[3]), start, stop), [ps], i, extra)

    def act(o, i, f, acc=None, bias=None, scale=None):
        kw = {}
        if bias is not None:
            kw["bias"] = ap(bias)
        if scale is not None:
            kw["scale"] = scale
        if acc is not None:
            kw["accum_out"] = ap(acc)
        op("s", lambda: S.activation(ap(o), ap(i), f, **kw), [o] + [s for s in (acc,) if s], [i] + [s for s in (bias,) if s])

    def iota(n, pattern, base=0, cm=0):
        kw = {} if SCRATCH[AT[n.split(":")[0]][0]][2] == "int32" else {"allow_small_or_imprecise_dtypes": True}
        op("g", lambda: g.iota(ap(n), pattern, base, cm, **kw), [n], [])

    def sel(o, i, pattern, cop, c, base, cm):
        op("g", lambda: g.affine_select(ap(o), ap(i), pattern, cop, c, base, cm), [o], [i])

    dma("dp", [("ys"[k % 2], T.PR[k:P:16, :], T.p[:, :]) for k in range(16)], ["PR"], [])
    dma("dx", [("y", T.X[:, :], T.x[:, :])], ["X"], [])
    dma("du", [("y", T.UT[:, :], T.u[:, :])], ["UT"], [])

    iota("QI:0:2", [[0, 2]], 0, 1)
    iota("C1", [[1, 20]])
    iota("E16", [[0, 20], [1, 16]])
    iota("JR", [[1, C]])
    iota("C16", [[16, 20]])
    iota("E32", [[0, 20], [1, 32]])
    iota("W", [[0, WW]], -160)
    fill("ZER", 0.0)
    fill("ONE", 1.0)
    dma("dz", [("y", T.D[:, a:min(a + 512, 3536)], T.ZER[:, 0:min(512, 3536 - a)]) for a in range(0, 3536, 512)], ["D"], ["ZER"])
    dma("dw", [("y", T.qL[:, 0:512].bitcast(dt.uint8), T.wc[:, :]), ("y", T.sL[:, 0:512], T.ws[:, :])], ["qL", "sL"], [])
    dma("dv", [("y", T.VT[:, :], T.v[:, :])], ["VT"], [])
    ts("QA:0:2", "QI:0:2", 15, A.bitwise_and)
    ts("QB:0:2", "QI:0:2", 4, A.arith_shift_right, 1, A.bitwise_and)
    cp("QP:0:1", "QA:0:1")
    cp("ODD:0:1", "QB:0:1")
    ts("Q20:0:1", "QP:0:1", 20.0, A.mult)
    ts("PERM", "C1", "Q20:0:1", A.add)
    ts("EVN:0:1", "ODD:0:1", -1.0, A.mult, 1.0, A.add)
    ts("NO:0:1", "ODD:0:1", float(NULL), A.mult)
    ts("NE:0:1", "EVN:0:1", float(NULL), A.mult)
    ts("MASK", "E16", "QP:0:1", A.is_equal)
    ts("RS", "E16", 0.0, A.is_gt)
    ts("MB0", "E16", "QP:0:1", A.is_lt)
    ts("CDF", "JR", -159.0, A.add)
    ts("MB", "MB0", 2.0 * BIG, A.mult, -BIG, A.add)
    ts("DUMP", "C16", "QP:0:1", A.add, 3600.0, A.add)
    fill("SKE", 3600.0 * 512.0)
    fill("ONES", 1.0)
    act("RS32", "E32", F.Sign)
    for b in range(4):
        sel("EB%d" % b, "ZER", [[1, 512]], A.not_equal, 1.0, -b, -4)
    iota("W2", [[0, 8 * C]])
    iota("UI", [[16, 8]])
    sel("OB1", "ONE", [[-16, 8], [0, 64]], A.is_ge, 0.0, 0, 1)
    sel("OB2", "OB1", [[16, 8], [0, 64]], A.is_ge, 0.0, 15, -1)
    cp("KF0", "PR@PERM")
    ts("KFB", "KF0", 512.0, A.mult, 512.0, A.add)
    tt("KFA", "KFB", "JR", A.add)

    def unpack():
        for b in range(4):
            mm("PF%d" % b, "E%d" % b, 0, "X")
        for b in range(4):
            act("FH%d" % b, "PF%d:0:320" % b, F.Copy, scale=0.5)

    def first_tiles():
        for b in range(4):
            quant("E%d" % b, "EB%d" % b)
        quant("X", "X")
        unpack()

    def sides():
        cp("UL", "UI")
        quant("U", "UT")
        quant("OB", "OB2")
        op("v", lambda: V.tensor_copy(T.qUR[:, 0:P].bitcast(dt.uint32), T.qU[:, 0:P].bitcast(dt.uint32).indirect(T.UL[:, 0:8])), ["qUR"], ["qU", "UL"])
        cp("sUR", "sU@UL")
        fill("TNY", 2.0 ** -126)
        ts("MSKA", "E16", "QP:0:1", A.is_le)

    def half(k):
        scan("VS%d" % k, "CMP%d:0:160" % k, "CMP%d:160:320" % k, 0.0, A.add, A.add)

    def spread(sem, a, b):
        moves = []
        for h in range(8):
            if h < 7:
                moves.append((T.D[16 * (h + 1) + h:P:16, a:b], T.CC[16 * h:16 * h + 7 - h, a:b]))
            if h:
                moves.append((T.D[h:16 * h:16, a + 1:b + 1], T.CC[16 * h + 8:16 * h + 8 + h, a:b]))
        dma(sem, [("ys"[k % 2], o, i) for k, (o, i) in enumerate(moves)], ["D:%d:%d" % (a, b)], ["CC:%d:%d" % (a, b)])

    def order(kf, joined, nv, during, scalar_tail):
        tt("KM", kf, "MASK", A.mult)
        scan("KS", "RS", "KM", 0.0, A.mult, A.add)
        for c in range(NS):
            act("JUNK%d" % c, kf, F.Sign, acc="ACC:%d:%d" % (c, c + 1), bias="KS:%d:%d" % (16 * c + 15, 16 * c + 16), scale=-1.0)
        n = 20 - NS
        for k in range(n):
            c = NS + k
            ts("CMP%d" % k, kf, "KS:%d:%d" % (16 * c + 15, 16 * c + 16), A.is_lt)
            if k:
                half(k - 1)
        half(n - 1)
        ts("RP:0:%d" % NS, "ACC:0:%d" % NS, 319.0, A.add, 0.5, A.mult)
        op("v", lambda: V.tensor_copy(ap("RP:%d:20" % NS), T.VSB[:, 159:160 * n:160]), ["RP:%d:20" % NS], ["VS%d" % k for k in range(n)])
        cp("SK@RP", kf)
        scan("S1", "SK", "MB", 0.0, A.min, A.max)
        op("v", lambda: V.tensor_tensor_scan(ap("S2"), T.SKB[:, 1:C + 1], ap("MB"), 0.0, A.min, A.max), ["S2"], ["SK", "SKE", "MB"])
        tt("SI:0:20", "S1:15:320:16", "SK:0:320:16", A.max)
        tt("SI:20:40", "S2:15:320:16", "SK:1:320:16", A.max)
        ts("SH", "SI", 9, A.arith_shift_right)
        tt("DU", "SH:0:20", "SH:20:40", A.is_equal)
        tt("DT", "DU", "DUMP", A.mult)
        tt("OW", "DT", "SH:0:20", A.max)
        cp("OWU", "OW")
        cp("W@OWU", "CDF")
        h = nv // 2
        lo, hi = "0:%d" % h, "%d:%d" % (h, nv)
        scan("CC:" + lo, "W:" + lo, "W:" + lo, -160.0, A.max, A.max)
        spread("dd", 0, h)
        scan("CC:" + hi, "W:" + hi, "W:" + hi, "CC:%d:%d" % (h - 1, h), A.max, A.max)
        spread("de", h, nv)
        scalar_tail()
        cp("KI", "KS:15:320:16")
        ts("RKP", "RP", 1120.0, A.add)
        ts("PI", "KI", 9, A.arith_shift_right)
        if joined:
            iota("W", [[0, WW]], -160)
            cp("OWD@RP", "JR")
        ts("OQ:0:40:2", "PI", "EVN:0:1", A.mult, "NO:0:1", A.add)
        ts("OQ:1:40:2", "PI", "ODD:0:1", A.mult, "NE:0:1", A.add)
        if joined:
            cp("OWD:320:321", "OWD:319:320")
            ts("O2", "OWD:0:320", 512.0, A.mult)
            tt("O3", "O2", "OWD:1:321", A.add)
        during()
        cp("G", "D@OQ")
        op("v", lambda: V.transpose(ap("GT"), ap("G")), ["GT"], ["G"])
        scan("GS", "RS32", "GT", 0.0, A.mult, A.add)
        tt("PL", "GS:31:640:32", "RKP", A.add)
        ts("C2I", "PL", 4, A.arith_shift_right)
        cp("C2OFF", "C2I")

    def lists1(again):
        cp("P2U", "PL")
        ts("CI", "PL", 3, A.arith_shift_right)
        cp("W2@P2U", "ONES")
        cp("COFF", "CI")
        scan("N2", "W2:0:2560:2", "W2:1:2560:2", -160.0, A.add, A.add)
        if again:
            iota("W2", [[0, 8 * C]])

    def lists2():
        scan("IX", "N2:3:1280:4", "MB", 0.0, A.min, A.max)
        tt("IXM", "IX:15:320:16", "N2:3:1280:64", A.max)
        ts("IXU", "IXM", 159.0, A.add, 0.0, A.max)
        tt("MM", "O3@IXU", "MASK", A.mult)
        scan("MS", "RS", "MM", 0.0, A.mult, A.add)
        ts("MJ", "MS:15:320:16", 2.0 ** -9, A.mult, -0.3125, A.add)
        cp("MI", "MS:15:320:16")
        cp("MOFF", "MJ")
        ts("NJ", "MI", 511, A.bitwise_and)
        cp("NOFF", "NJ")

    order("KFA", True, 2576, first_tiles, lambda: None)
    lists1(True)
    names = ["KFA", "KFB"]
    for t in range(R):
        last = t == R - 1
        lists2()
        qz = "Z%d" % t
        for b in range(4):
            act("GB%d" % b, "FH%d@MOFF" % b, F.Copy)
        if t == 0:
            sides()
        for b in range(4):
            tt("Z:%d:1280:4" % b, "FH%d@NOFF" % b, "GB%d" % b, A.add)
        quant(qz, "Z")
        wait("g", [x[1:] for x in wr["q" + qz] + wr["s" + qz]])
        rid, pid, _s = topo.addr(nxt)
        m, arr = topo.mask(core, nxt), "arr%d" % t
        n = 2 * len(topo.engines(core, nxt))
        g.remote_dma(T["qA%d" % t][:, 0:C].bitcast(dt.uint8), T["q" + qz][:, 0:C].bitcast(dt.uint8), T.sem[arr], T.sem.sent, pid, rid, m)
        g.remote_dma(T["sA%d" % t][:, 0:C], T["s" + qz][:, 0:C], T.sem[arr], T.sem.sent, pid, rid, m)
        cnt["sent"], cnt[arr] = cnt.get("sent", 0) + n, n
        mm("PS", "UR", 0, qz)
        mm("PSB", "UR", 0, qz)
        tt("SM", "PS:0:320", "MASK", A.mult)
        act("DD", "PSB:0:320", F.Abs, bias="TNY", scale=1.01 * 2.0 ** -24)
        scan("SS", "RS", "SM", 0.0, A.mult, A.add)
        tt("DM", "DD", "MSKA", A.mult)
        keys = "SS:%d:320:16" % (CS + 15)
        act("NA", keys, F.Abs, bias="TNY", scale=1.01 * 2.0 ** -24)
        tt("RA", "PS:0:320", "DM", A.subtract)
        tt("ND", keys, "NA", A.subtract)
        for w in range(WS, 5):
            for e in range(4):
                a = 4 * w + e
                s, ct, d = "SS:%d:%d" % (16 * a + 15, 16 * a + 16), "CT%d:%%d:%%d:4" % w, "ND:%d:%d" % (a - 4 * WS, a - 4 * WS + 1)
                if a:
                    act(ct % (e, 64 * a), "PSB:0:%d" % (16 * a), F.Sign, bias=s, scale=-1.0)
                act(ct % (64 * a + e, 64 * a + 64), "RA:%d:%d" % (16 * a, 16 * a + 16), F.Sign, bias=d, scale=-1.0)
                if a < 19:
                    act(ct % (64 * a + 64 + e, 4 * C), "PSB:%d:320" % (16 * a + 16), F.Sign, bias=d, scale=-1.0)
            act("CT%d" % w, "CT%d" % w, F.Relu, scale=-1.0)
        for w in range(5):
            for e in range(4 if w < WS else 0):
                a = 4 * w + e
                s, ct = "SS:%d:%d" % (16 * a + 15, 16 * a + 16), "CT%d:%%d:%%d:4" % w
                if a:
                    ts(ct % (e, 64 * a), "PS:0:%d" % (16 * a), s, A.is_gt)
                ts(ct % (64 * a + e, 64 * a + 64), "RA:%d:%d" % (16 * a, 16 * a + 16), s, A.is_ge)
                if a < 19:
                    ts(ct % (64 * a + 64 + e, 4 * C), "PS:%d:320" % (16 * a + 16), s, A.is_ge)
            quant("C%d" % w, "CT%d" % w)
            mm("PK", "OB", 0, "C%d" % w, w == 0, w == 4)
        act("STEP", "PK:0:320", F.Copy, scale=512.0)
        old, new = names[t % 2], names[(t + 1) % 2]
        tt(new, "STEP@COFF", old, A.add)

        def deal(t=t, arr=arr):
            banks = ("PH", "PS", "PSB", "PK")
            for b in range(4):
                mm(banks[b], "L", P * b, "A%d" % t, extra=[(arr, cnt[arr])])
            for b in range(4):
                act("HB%d" % b, banks[b] + ":1:320:2", F.Copy, scale=0.03125)

        def final(new=new):
            if last:
                tt("PT0", new, "JR", A.subtract)
                ts("PT1", "PT0", 2.0 ** -9, A.mult, -1.0, A.add)
                quant("V", "VT")

        order(new, not last, (2896, 3216, NV)[t], final, deal)
        if last:
            dma("dpt", [("y", T.pt[:, :], T.PT1[0:P:16, :])], [], ["PT1"])
        for b in range(4):
            if last and b > 1:
                cp("GB%d" % b, "HB%d@C2OFF" % b)
            else:
                act("GB%d" % b, "HB%d@C2OFF" % b, F.Copy)
        if not last:
            lists1(t + 1 < R - 1)
        for b in range(4):
            tt("X:%d:1280:4" % b, "GB%d" % b, "PF%d:0:320" % b, A.add)
        quant("X", "X")
        if not last:
            unpack()

    mm("PS", "V", 0, "X")
    dma("dout", [("y", T.oc[:, :], T.qX[:, 0:C].bitcast(dt.uint8))] +
        [("ys"[k % 2], T.osc[4 * k:4 * k + 4, :], T.sX[32 * k:32 * k + 4, 0:C]) for k in range(4)], [], ["qX", "sX"])
    act("YB", "PS:0:320", F.Copy)
    dma("dy", [("s", T.y[:, :], T.YB[:, :])], [], ["YB"])
    wait("g", list(cnt.items()))
